import numpy as np, ml_dtypes
CORES = [40,64,80,88,96,104,120,144]
N = 8
import mx_ref
BF = ml_dtypes.bfloat16
def gentries(a):
    return np.ascontiguousarray(a.reshape(8, 16, -1).transpose(0, 2, 1)).reshape(8, -1)
def gtable(e):
    e = np.asarray(e); return np.ascontiguousarray(e.reshape(8, -1, 16).transpose(0, 2, 1)).reshape(128, -1).astype(np.int32)
def gcols(t, e):
    v = np.concatenate([t.reshape(8, 16, -1, 4), np.zeros((8, 16, 1, 4), BF)], axis=2)
    return np.ascontiguousarray(np.stack([v[g][:, e[g]] for g in range(8)])).reshape(128, -1)
def tile(rs):
    return np.stack(rs, axis=2).reshape(128, -1).astype(BF)
def pick(q, e):
    c = np.concatenate([q[0].reshape(128, -1, 4), np.zeros((128, 1, 4), np.uint8)], axis=1); s = np.concatenate([q[1], np.ones((16, 1), np.uint8)], axis=1)
    return (np.ascontiguousarray(c[:, e].reshape(128, -1)), np.ascontiguousarray(s[:, e]))
def join(*qs):
    return (np.concatenate([q[0] for q in qs], axis=1), np.concatenate([q[1] for q in qs], axis=1))
def put(q, e, v):
    c, s = q[0].reshape(128, -1, 4).copy(), q[1].copy(); c[:, e] = v[0].reshape(128, -1, 4); s[:, e] = v[1]
    return (c.reshape(128, -1), s)
def pk(c, s):
    return (np.ascontiguousarray(c), mx_ref.live(s))
def emit(q):
    return q[0], q[1]
def packed(v, rng):
    q = [mx_ref.quantize(np.ascontiguousarray(v[r])) for r in range(N)]
    return np.stack([a for a, b in q]), np.stack([mx_ref.plane(b, rng) for a, b in q])
def values_of_codes():
    e, c = np.zeros((128, 128, 4), np.float32), np.zeros((128, 2, 4), np.uint8)
    e[np.arange(128), np.arange(128), 0] = 1
    c[:127, :, 0] = np.arange(256).reshape(2, 128).T[:127]
    return mx_ref.matmul(mx_ref.quantize(e.reshape(128, 512).astype(BF)), (c.reshape(128, 8), np.full((16, 2), 127, np.uint8))).T.reshape(-1).astype(np.float64)
CODE_VALUE, SCALE_VALUE = values_of_codes(), 2.0 ** (np.arange(256) - 127.0)
def decode(q):
    return (CODE_VALUE[q[0]].reshape(16, 8, -1, 4) * SCALE_VALUE[q[1]][:, None, :, None] + 0.0).reshape(128, -1).astype(np.float32)
def f(rng, *shape):
    return mx_ref.flush((rng.standard_normal(shape, dtype=np.float32) * np.exp2(rng.integers(-2, 3, shape[:-1] + (1,)))).astype(BF))
def wide(rng, *shape, cols=0):
    v = rng.standard_normal(shape, dtype=np.float32) * np.exp2(rng.integers(-12, 13, shape)).astype(np.float32)
    if cols: v *= np.repeat(np.exp2(rng.integers(-cols, cols + 1, shape[:-2] + (1, shape[-1] // 4))) * (rng.random(shape[:-2] + (1, shape[-1] // 4)) > 0.0625), 4, axis=-1).astype(np.float32)
    return mx_ref.flush(v.astype(BF))
C, GW, R, SWEEPS = 256, 64, 3, 6
JUMP = [0, 1, 4]
def big(v):
    v = v.astype(np.float32)
    v[np.abs(v) < np.float32(2.0 ** -16)] = 0
    return v.astype(BF)
def numbers_of(rng):
    return {"x": big(f(rng, N, 128, 4 * C)), "u": np.array(f(rng, N, 128, 512)), "v": np.array(f(rng, N, 128, 512))}
def weights(rng, still=[]):
    w = big(f(rng, N, 128, 2048)).reshape(N, 8, 16, 4, 8, 16, 4)
    for i in still:
        w[:, :, i] = 0
        w[:, :, :, :, :, i] = 0
    c, p = packed(w.reshape(N, 128, 2048), rng)
    return {"wc": c, "ws": p}
def ltable(a):
    return gtable(a.transpose(1, 0, 2).reshape(8, 3 * C))
def drawn(rng):
    a = np.zeros((3, 8, C), np.int64)
    for g in range(8):
        o = rng.permutation(C)
        a[0, g, o[::2]] = o[1::2]
        a[0, g, o[1::2]] = o[::2]
        for k in (1, 2):
            if g & JUMP[k] == 0:
                o = rng.permutation(C)
                a[k, g] = o
                a[k, g ^ JUMP[k], o] = np.arange(C)
    return a
def links(rng):
    return np.stack([ltable(drawn(rng)) for r in range(N)])
def setup_inputs(rng):
    return {**numbers_of(rng), "lk": links(rng), **weights(rng)}
def setup_inputs_ties(rng):
    d = numbers_of(rng)
    x = d["x"].reshape(N, 8, 16, C, 4)
    x[:, :, 0] = 0
    x[:, :, 0, :, 0] = rng.integers(0, 4, (N, 8, C)).astype(np.float32).astype(BF)
    u = d["u"].reshape(N, 128, 128, 4)
    u[:, :, ::16] = 0
    o = rng.permutation(N)
    for r in range(N):
        for h in range(0, 128, 16): u[r, h, h, 0] = 0.0 if r == o[0] else -1.0 if r == o[1] else 1.0
    return {"x": x.reshape(N, 128, 4 * C), "u": u.reshape(N, 128, 512), "v": d["v"], "lk": links(rng), **weights(rng, [0])}
def setup_inputs_near(rng):
    d = numbers_of(rng)
    x = d["x"].astype(np.float32).reshape(N, 8, 16, C, 4)
    x[:, :, 0] = 0
    x[:, :, 8:] = 0
    x[:, :, 0, :, 0] = 1
    s = rng.integers(0, 16, (N, 8, C))
    x[:, :, 8] = ((s[:, :, :, None] >> np.arange(4)) & 1) * np.exp2(np.arange(4) - 21.0)
    x[:, :, 11, :, 0] = 2.0 ** -10
    u = d["u"].reshape(N, 128, 128, 4)
    u[:, :, ::16] = 0
    o = rng.permutation(N) % 4
    for r in range(N):
        far = rng.permutation(8)
        if o[r] == 0: x[r, :, 0, :, 0] = 7
        if o[r] == 1: x[r, :, 0, :, 0] = -1
        if o[r] < 2:
            for i in range(4): x[r, far[i], 0, rng.integers(C), 0] = (-1.5 if i == 0 else 1.5) * 2.0 ** 29
        if o[r] == 3:
            x[r, :, 8:] = 0
            x[r, :, 10, :, 0] = (8 + rng.integers(0, 8, (8, C))) * 2.0 ** -33
        k = 1.0 if o[r] == 0 else 2.0 ** -30
        for g in range(8):
            h = 16 * g
            if o[r] < 2:
                u[r, h, h, 0] = k
                u[r, h + 11, h, 0] = k
            if o[r] == 2 and g == far[0]: u[r, h, h, 0] = 1.0
            if o[r] == 2 and g == far[1]: u[r, h, h, 0] = -1.0
            if o[r] < 3: u[r, h + 8, h] = k
            else: u[r, h + 10, h, 0] = k * 1.125 if g >= 4 else k
    return {"x": x.reshape(N, 128, 4 * C).astype(BF), "u": u.reshape(N, 128, 512), "v": d["v"], "lk": links(rng), **weights(rng, [0, 8, 9, 10, 11, 12, 13, 14, 15])}
def setup_inputs_cubes(rng):
    d = numbers_of(rng)
    x = d["x"].reshape(N, 8, 16, C, 4)
    x[:, :, 0] = 0
    low = (1.125 + 0.25 * rng.integers(0, 4, (N, 8, 8, C, 4))) * np.exp2(10.0 - rng.integers(8, 15, (N, 8, 8, C, 4)))
    x[:, :, 8:] = (low * rng.choice([-1.0, 1.0], (N, 8, 8, C, 4))).astype(np.float32).astype(BF)
    x[:, :, 8, :, 0] = 2016.0
    u = d["u"].reshape(N, 128, 128, 4)
    u[:, :, ::16] = 0
    p, e = [], rng.permutation(N)
    for r in range(N):
        o = rng.permutation(C) if e[r] % 2 else np.arange(C)
        k = np.zeros(C, np.float32)
        k[o] = np.repeat(rng.integers(-7, 8, C // 2), 2)
        x[r, :, 0, :, 0] = k.astype(BF)
        a = np.tile(np.arange(C), (3, 8, 1))
        a[0][:, o] = o[np.arange(C) ^ 1]
        p.append(ltable(a))
        for h in range(0, 128, 16): u[r, h, h, 0] = -1.0 if e[r] == 0 else 1.0
    w = big(f(rng, N, 128, 2048)).reshape(N, 8, 16, 4, 8, 16, 4)
    w[:, :, 0] = 0
    w[:, :, 8, :, :, :, 0] = 0
    w[:, :, :, :, :, 0] = 0
    w[:, :, :, :, :, 8:] = 0
    for g in range(8): w[:, g, 8, 0, g, 8, 0] = -1.0
    c, s = packed(w.reshape(N, 128, 2048), rng)
    return {"x": x.reshape(N, 128, 4 * C), "u": u.reshape(N, 128, 512), "v": d["v"], "lk": np.stack(p), "wc": c, "ws": s}
def setup_inputs_ends(rng):
    d = numbers_of(rng)
    o = rng.permutation(N) % 4
    a, b = np.flatnonzero(o < 2)[:2]
    o[[a + 1, b]] = o[[b, a + 1]]
    sg = rng.choice([-1.0, 1.0], N)
    x = np.ones((N, 8, 16, C, 4))
    u = d["u"].astype(np.float32).reshape(N, 8, 16, 8, 16, 4)
    u[:, :, :, :, 0] = 0
    v = rng.choice([-1.0, 1.0], (N, 128, 512))
    w = np.zeros((N, 128, 4, 128, 4), np.float32)
    i, p = np.arange(128), []
    for r in range(N):
        large = o[r] < 2
        size = 2.0 ** 30 if large else 2.0 ** -30
        h = rng.permutation(8)
        x[r, h[4:]] = rng.choice([1.0, 0.875, 0.75] if large else [1.0, 1.125, 1.25], (4, 1, C, 1))
        x[r] *= sg[r] * size
        v[r] *= size
        k = size * sg[r] * (1.0 if o[r] % 2 == 0 else -1.0)
        for g in range(8):
            for c in (h[:4] if g in h[:4] else h): u[r, c, :, g, 0] = k
        for b in range(4): w[r, i, b, i, b] = sg[r] * sg[r - 1] * (-2.0 if large else 2.0)
        a = drawn(rng)
        if large:
            a[:2] = C - 1 - np.arange(C)
            a[2] = np.arange(C)
        p.append(ltable(a))
    c, s = packed(w.reshape(N, 128, 2048).astype(BF), rng)
    return {"x": x.reshape(N, 128, 4 * C).astype(np.float32).astype(BF), "u": u.reshape(N, 128, 512).astype(BF), "v": v.astype(np.float32).astype(BF), "lk": np.stack(p), "wc": c, "ws": s}
def setup_inputs_spread(rng):
    d = setup_inputs(rng)
    d["x"] = big(wide(rng, N, 128, 4 * C, cols=6))
    return d
def check_inputs(d):
    b = []
    for k in ("x", "u", "v"):
        a = np.abs(d[k].astype(np.float32))
        if not (np.isfinite(a).all() and ((a == 0) | (a >= 2.0 ** -30) & (a <= 2.0 ** 30)).all()): b.append("a value of " + k)
    none, least, most = [emit(mx_ref.quantize(np.full((128, 16), k, np.float32).astype(BF)))[1][0, 0] for k in (0.0, 2.0 ** -16, 2.0 ** 5)]
    for r in range(N):
        e = gentries(d["lk"][r])
        if not ((e >= 0) & (e < C)).all(): b.append("an entry of lk")
        else:
            n = other_ends(d["lk"][r])
            if (np.take_along_axis(n, n, axis=1) != np.arange(8 * C)).any(): b.append("a link of lk isn't the same from both ends")
            if (n == np.arange(8 * C)).any(): b.append("a link of lk from a node to itself")
        if ((d["wc"][r] == 0x7F) | (d["wc"][r] == 0xFF)).any(): b.append("wc: a code that is no number")
        s = mx_ref.live(d["ws"][r])
        if ((s != none) & ((s < least) | (s > most))).any(): b.append("ws: a scale out of range")
    return b
def other_ends(a):
    e = gentries(a).reshape(8, 3, C).astype(np.int64)
    return np.stack([(e[:, k] + C * (np.arange(8) ^ JUMP[k])[:, None]).reshape(-1) for k in range(3)])
def parts(t):
    return t.reshape(8, 16, -1, 4).transpose(0, 2, 1, 3).reshape(-1, 16, 4)
def whole(p):
    return np.ascontiguousarray(p.reshape(8, -1, 16, 4).transpose(0, 2, 1, 3)).reshape(128, -1)
def reference(x, u, v, lk, wc, ws):
    qu = [mx_ref.quantize(u[r]) for r in range(N)]
    lay = [pk(wc[r], ws[r]) for r in range(N)]
    ends = [other_ends(lk[r]) for r in range(N)]
    now = [x[r] for r in range(N)]
    node = np.arange(8 * C)
    away, mark = [None] * N, [np.zeros((3, 8 * C), bool) for r in range(N)]
    route = [None] * N
    for t in range(R):
        sent, blend, gate = [], [], []
        for r in range(N):
            q, n = mx_ref.quantize(now[r]), ends[r]
            s = mx_ref.matmul(qu[r], q)[::16] + np.float32(0.0)
            l = np.argsort(s, axis=1, kind="stable")[:, :GW]
            slot = np.full((8, C), -1)
            np.put_along_axis(slot, l, np.tile(np.arange(GW), (8, 1)), axis=1)
            slot, s = slot.reshape(-1), s.reshape(-1)
            a, m = away[r], mark[r]
            if t == 0: a = (s[n] < s) | (s[n] == s) & (n < node)
            for i in range(SWEEPS):
                sink = ~a.any(axis=0) & (slot < 0)
                turn = sink & (~m | m.all(axis=0))
                came = np.take_along_axis(turn, n, axis=1)
                a = (a | turn) & ~came
                m = (m & ~sink) | came
            away[r], mark[r] = a, m
            k = np.argmin(np.where(a, s[n], np.float32(np.inf)), axis=0)
            to = np.where((slot < 0) & a.any(axis=0), n[k, node], node)
            e = to[to]
            e = e[e]
            own = decode(q)
            p = parts(own)
            blend.append(((p[to] + p[e]) * np.float32(0.5)).astype(BF))
            sent.append(mx_ref.quantize(gcols(own.astype(BF), l)))
            gate.append(slot)
            route[r] = e
        for r in range(N):
            h = parts(tile([mx_ref.matmul(pick(lay[r], np.arange(128 * b, 128 * b + 128)), sent[r - 1]) * np.float32(0.015625) for b in range(4)]))
            z, e, k = blend[r], route[r], gate[r][route[r]]
            w = k >= 0
            z[w] = (z[w].astype(np.float32) + h[GW * (e[w] // C) + k[w]].astype(np.float32)).astype(BF)
            now[r] = whole(z)
    y, nd = np.zeros((N, 128, C), np.float32), np.zeros((N, 8, 2 * C), np.float32)
    oc, osc = np.zeros((N, 128, 4 * C), np.uint8), np.zeros((N, 16, C), np.uint8)
    for r in range(N):
        q = mx_ref.quantize(now[r])
        y[r] = mx_ref.matmul(mx_ref.quantize(v[r]), q)
        nd[r, :, :C] = route[r].reshape(8, C)
        a, m = away[r].astype(np.int64), mark[r].astype(np.int64)
        nd[r, :, C:] = (a[0] + 2 * a[1] + 4 * a[2] + 8 * m[0] + 16 * m[1] + 32 * m[2]).reshape(8, C)
        oc[r], osc[r] = emit(q)
    return {"y": y, "nd": nd, "oc": oc, "osc": osc}

@@ -1,0 +1,601 @@
+from concourse.bass import IndirectOffsetOnAxis
+from concourse.mybir import dt, AluOpType, AxisListType, ActivationFunctionType
+
+N, C, GW, ROUNDS, SWEEPS = 8, 256, 64, 3, 6
+F8, F32, BF, I32, U16, U8 = "float8_e4m3fn_x4", "float32", "bfloat16", "int32", "uint16", "uint8"
+SCRATCH = {
+    "xt": ("sbuf", [128, 1024], BF), "xn": ("sbuf", [128, 1024], BF), "ut": ("sbuf", [128, 512], BF), "vt0": ("sbuf", [128, 512], BF),
+    "lki": ("sbuf", [128, 48], I32), "lku": ("sbuf", [128, 48], U16), "lkf": ("sbuf", [128, 48], F32), "lkx": ("sbuf", [128, 64], F32),
+    "tbl": ("dram", [4, 2048], F32), "l4": ("sbuf", [128, 4096], F32), "tbh": ("dram", [4, 512], F32), "ho": ("sbuf", [128, 1024], F32),
+    "xq": ("sbuf", [128, 256], F8), "xs": ("sbuf", [128, 256], U8), "uq": ("sbuf", [128, 128], F8), "us": ("sbuf", [128, 128], U8),
+    "up": ("sbuf", [128, 384], F8), "ups": ("sbuf", [128, 384], U8), "vq": ("sbuf", [128, 128], F8), "vs": ("sbuf", [128, 128], U8),
+    "wq": ("sbuf", [128, 512], F8), "wsx": ("sbuf", [128, 512], U8), "wp": ("sbuf", [128, 2048], F8), "wps": ("sbuf", [128, 2048], U8),
+    "ci": ("sbuf", [128, 16], I32), "cf": ("sbuf", [128, 64], F32), "jm": ("sbuf", [128, 256], F32), "jd": ("sbuf", [128, 128], F32),
+    "jrow": ("sbuf", [128, 256], F32), "gx": ("sbuf", [128, 128], F32), "gc": ("sbuf", [128, 128], F32), "ta": ("sbuf", [128, 128], F32),
+    "ulf": ("sbuf", [128, 24], F32), "ul": ("sbuf", [128, 24], U16), "wlf": ("sbuf", [128, 128], F32), "wl": ("sbuf", [128, 128], U16),
+    "t16": ("sbuf", [128, 16], F32), "l15": ("sbuf", [128, 16], U16), "m0": ("sbuf", [128, 16], U16), "ql": ("sbuf", [128, 8], U16),
+    "coff": ("sbuf", [128, 64], F32), "vlf": ("sbuf", [128, 8], F32), "vl": ("sbuf", [128, 8], U16), "vr": ("sbuf", [128, 128], F32),
+    "vm": ("sbuf", [128, 128], F32), "mask": ("sbuf", [128, 256], F32), "rst": ("sbuf", [128, 256], F32), "pen": ("sbuf", [128, 256], F32),
+    "oh": ("sbuf", [128, 16], F32), "rb": ("sbuf", [128, 192], F32), "mm3": ("sbuf", [128, 8], F32), "blkx": ("sbuf", [128, 128], F32),
+    "kc": ("sbuf", [128, 128], BF), "kp": ("sbuf", [128, 128], BF), "kt": ("sbuf", [128, 3584], BF), "kq": ("sbuf", [128, 896], F8), "ks": ("sbuf", [128, 896], U8),
+    "zc": ("sbuf", [128, 512], BF), "ke0": ("sbuf", [128, 2048], BF), "ke1": ("sbuf", [128, 2048], BF),
+    "keq": ("sbuf", [128, 2048], F8), "kes": ("sbuf", [128, 2048], U8), "lt0": ("sbuf", [128, 256], F32),
+    "sw": ("sbuf", [128, 768], F32), "nn": ("sbuf", [128, 768], F32), "nt": ("sbuf", [128, 768], F32), "pw": ("sbuf", [128, 96], F32),
+    "so": ("sbuf", [128, 256], F32), "wsc": ("sbuf", [128, 256], F32), "wm": ("sbuf", [128, 256], F32), "dtl": ("sbuf", [128, 1024], BF),
+    "cm0": ("sbuf", [128, 1024], BF), "cm1": ("sbuf", [128, 1024], BF), "cq": ("sbuf", [128, 1280], F8), "cs": ("sbuf", [128, 1280], U8),
+    "ct": ("sbuf", [128, 1024], BF), "ct2": ("sbuf", [128, 1024], BF), "cc": ("sbuf", [128, 1024], BF), "ctq": ("sbuf", [128, 512], F8), "cts": ("sbuf", [128, 512], U8),
+    "ccq": ("sbuf", [128, 256], F8), "ccs": ("sbuf", [128, 256], U8), "dh": ("sbuf", [128, 256], F32), "dh2": ("sbuf", [128, 256], F32),
+    "bw": ("sbuf", [128, 256], BF), "st": ("sbuf", [128, 1024], BF), "sq": ("sbuf", [128, 256], F8), "ss": ("sbuf", [128, 256], U8),
+    "bt": ("sbuf", [128, 256], BF), "tk": ("sbuf", [128, 80], F32), "eqk": ("sbuf", [128, 32], F32), "vt": ("sbuf", [128, 512], BF),
+    "vtq": ("sbuf", [128, 128], F8), "vts": ("sbuf", [128, 128], U8), "of": ("sbuf", [128, 64], F32), "ou": ("sbuf", [128, 64], U16),
+    "da": ("sbuf", [128, 1024], F32), "hp": ("sbuf", [128, 256], F32), "hs": ("sbuf", [128, 256], F32), "mu": ("sbuf", [128, 128], U16),
+    "rr": ("sbuf", [128, 256], F32), "r1": ("sbuf", [128, 256], F32), "r2": ("sbuf", [128, 256], F32), "lw": ("sbuf", [128, 256], F32),
+    "fw": ("sbuf", [128, 4096], BF), "hw": ("sbuf", [128, 4096], BF), "fd": ("sbuf", [128, 1024], BF), "zb": ("sbuf", [128, 1024], BF),
+    "et": ("sbuf", [128, 512], BF), "zq": ("sbuf", [128, 128], F8), "zs": ("sbuf", [128, 128], U8),
+    "ys": ("sbuf", [128, 256], F32), "ndb": ("sbuf", [128, 512], F32), "ev": ("sbuf", [128, 512], F32),
+}
+SCRATCH["pb"] = ("psum", [128, 4096], F32)
+for _n, _w in (("e", 128), ("r", GW), ("a", 128)):
+    SCRATCH[_n + "q"] = ("sbuf", [128, _w * ROUNDS], F8)
+    SCRATCH[_n + "s"] = ("sbuf", [128, _w * ROUNDS], U8)
+PIECE = {}
+for _n, _w, _k in (("pb", 512, 8), ("sw", 256, 3), ("n", 256, 3), ("nt", 256, 3), ("eq", 128, 3), ("es", 128, 3), ("rq", GW, 3), ("rs", GW, 3), ("aq", 128, 3), ("as", 128, 3)):
+    for _i in range(_k):
+        PIECE["%s%d" % (_n, _i)] = ("nn" if _n == "n" else _n, _w * _i)
+SEMAPHORES = ["qv", "qa", "qt", "qp", "loc"] + ["arr%d" % i for i in range(ROUNDS)] + ["rel%d" % i for i in range(ROUNDS)] + ["d%d" % i for i in range(48)]
+NE = 4
+
+
+def view(T, n, a, b, st=1):
+    n, o = PIECE.get(n, (n, 0))
+    return T[n][:, o + a:o + b] if st == 1 else T[n][:, o + a:o + b:st]
+
+
+def mask_of(topo, src, dst):
+    return sum(1 << e for e in topo.engines(src, dst)[:NE])
+
+
+def helper_of(topo, src, dst):
+    if topo.may_write(src, dst):
+        return None
+    able = [c for c in topo.cores_of(src) if c != src and topo.may_write(c, dst)]
+    near = [c for c in able if topo.die(c) == topo.die(src)]
+    return (near or able)[0]
+
+
+def send(g, T, topo, src, dst, q_out, q_in, s_out, s_in, sem):
+    rid, pid = topo.addr(dst, src)
+    m = mask_of(topo, src, dst)
+    g.remote_dma(q_out.bitcast(dt.uint8), q_in.bitcast(dt.uint8), sem, T.sem.loc, pid, rid, m)
+    g.remote_dma(s_out, s_in, sem, T.sem.loc, pid, rid, m)
+
+
+def rank_program(g, core, T, topo):
+    rank = T.rank_of(core)
+    if rank is None:
+        n = 0
+        for i in range(N):
+            src, dst = T.cores[i], T.cores[(i + 1) % N]
+            if helper_of(topo, src, dst) != core:
+                continue
+            for t in range(ROUNDS):
+                g.wait_ge(T.sem["rel%d" % t], 2 * NE)
+                send(g, T, topo, core, dst, view(T, "aq%d" % t, 0, GW), view(T, "rq%d" % t, 0, GW), view(T, "as%d" % t, 0, GW), view(T, "rs%d" % t, 0, GW), T.sem["arr%d" % t])
+                n += 2 * NE
+        if n:
+            g.wait_ge(T.sem.loc, n)
+        return
+
+    A, AF = AluOpType, ActivationFunctionType
+    Q = {"v": g.vector, "a": g.scalar, "t": g.tensor, "g": g, "s": g.sync}
+    SRC = {"v": "qv", "a": "qa", "t": "qt", "g": "qp"}
+    cnt = {}
+    known = {q: {} for q in Q}
+    clk = {}
+    wrote, read = {}, {}
+    ndma = [0]
+
+    def waits(q, rd, wr, free=False):
+        need = {}
+
+        def want(e):
+            if e[0] == SRC.get(q) and (free or q == "t"):
+                return
+            if need.get(e[0], 0) < e[1]:
+                need[e[0]] = e[1]
+        for r in rd:
+            if r in wrote:
+                e = wrote[r]
+                if not (e[0] == SRC.get(q) and q == "t"):
+                    if need.get(e[0], 0) < e[1]:
+                        need[e[0]] = e[1]
+            if r[:2] == "pb":
+                for s, k in read.get(r, {}).items():
+                    if s != SRC.get(q):
+                        want((s, k))
+        for w in wr:
+            if w in wrote:
+                want(wrote[w])
+            for s, k in read.get(w, {}).items():
+                want((s, k))
+        need = {s: k for s, k in need.items() if known[q].get(s, 0) < k}
+        for s, k in sorted(need.items()):
+            if any(s2 != s and clk[(s2, k2)].get(s, 0) >= k for s2, k2 in need.items()):
+                continue
+            Q[q].wait_ge(T.sem[s], k)
+        for s, k in need.items():
+            for s2, k2 in clk[(s, k)].items():
+                if known[q].get(s2, 0) < k2:
+                    known[q][s2] = k2
+            if known[q].get(s, 0) < k:
+                known[q][s] = k
+
+    def done(e, rd, wr, q):
+        clk[e] = dict(known[q])
+        for r in rd:
+            read.setdefault(r, {})[e[0]] = e[1]
+        for w in wr:
+            wrote[w] = e
+            read[w] = {}
+
+    def op(q, fn, rd, wr, free=False):
+        waits(q, rd, wr, free)
+        s = SRC[q]
+        cnt[s] = cnt.get(s, 0) + 1
+        fn(Q[q]).then_inc(T.sem[s], 1)
+        done((s, cnt[s]), rd, wr, q)
+
+    def dma(q, fn, rd, wr):
+        waits(q, rd, wr)
+        s = "d%d" % ndma[0]
+        ndma[0] += 1
+        cnt[s] = 16
+        fn(Q[q]).then_inc(T.sem[s], 16)
+        done((s, 16), rd, wr, q)
+
+    def V(n, a, b, st=1):
+        return view(T, n, a, b, st)
+
+    def lanes(n, *ls):
+        return [n + "." + str(x) for x in (ls or (0, 1, 2, 3))]
+
+    def ts(out, in0, s1, o0, s2=None, o1=None, rd=(), wr=(), free=False):
+        if s2 is None:
+            op("v", lambda e: e.tensor_scalar(out, in0, s1, None, o0), list(rd), list(wr), free)
+        else:
+            op("v", lambda e: e.tensor_scalar(out, in0, s1, s2, o0, o1), list(rd), list(wr), free)
+
+    def tt(out, a, b, o, rd=(), wr=(), free=False):
+        op("v", lambda e: e.tensor_tensor(out, a, b, o), list(rd), list(wr), free)
+
+    def vc(out, in_, rd=(), wr=(), free=False):
+        op("v", lambda e: e.tensor_copy(out, in_), list(rd), list(wr), free)
+
+    def act(out, in_, rd=(), wr=(), scale=1.0, bias=None):
+        if bias is None:
+            op("a", lambda e: e.activation(out, in_, AF.Copy, scale=scale), list(rd), list(wr))
+        else:
+            op("a", lambda e: e.activation(out, in_, AF.Identity, bias=bias, scale=scale), list(rd), list(wr))
+
+    def iota(n, a, b, pat, base=0, cm=0, st=1):
+        f = SCRATCH[n][2] == F32
+        if f:
+            op("g", lambda e: e.iota(V(n, a, b, st), pat, base, cm, allow_small_or_imprecise_dtypes=True), [], [n], True)
+        else:
+            op("g", lambda e: e.iota(V(n, a, b, st), pat, base, cm), [], [n], True)
+
+    def zero(n, rd, wr):
+        op("v", lambda e: e.memset(T[n][:], 0.0), rd, wr)
+
+    def quant(cq, cs, a, b, tile, rd, wr, ta=0):
+        op("v", lambda e: e.quantize_mx(V(cq, a, b), V(cs, a, b), V(tile, ta, ta + 4 * (b - a))), rd, wr)
+
+    def mm(bank, n, lq, ls, la, rq, rs, ra, start, stop, rd):
+        op("t", lambda e: e.matmul_mx(V("pb%d" % bank, 0, n), V(lq, la, la + 128), V(ls, la, la + 128), V(rq, ra, ra + n), V(rs, ra, ra + n), start, stop),
+           rd, ["pb%d" % bank])
+
+    def ind(n, a, b, off, oa, ob):
+        return V(n, a, b).indirect(V(off, oa, ob))
+
+    K = {"own": 0, "pl": 128, "init": 256, "s": 384, "fin": 512, "kw": 640, "nd": 768}
+
+    dma("s", lambda e: e.dma_start(T.ut[:], T.u[:, :]), [], ["ut"])
+    dma("a", lambda e: e.dma_start(T.xt[:], T.x[:, :]), [], ["xt"])
+    dma("s", lambda e: e.dma_start(T.lki[:], T.lk[:, :]), [], ["lki"])
+    dma("a", lambda e: e.dma_start(T.wq[:].bitcast(dt.uint8), T.wc[:, :]), [], ["wq"])
+    dma("s", lambda e: e.dma_start(T.wsx[:], T.ws[:, :]), [], ["wsx"])
+    dma("s", lambda e: e.dma_start(T.vt0[:], T.v[:, :]), [], ["vt0"])
+
+    iota("ci", 0, 1, [[0, 1]], 0, 1)
+    iota("jm", 0, 256, [[0, 16], [1, 16]])
+    iota("ulf", 0, 8, [[16, 8]])
+    iota("ulf", 8, 16, [[32, 4], [-16, 2]], 16)
+    iota("ulf", 16, 24, [[-64, 2], [16, 4]], 64)
+    iota("gx", 0, 128, [[1, 8], [0, 16]])
+    op("g", lambda e: e.iota(V("gx", 13, 128, 16), [[2, 4], [-1, 2]], 1, 0, allow_small_or_imprecise_dtypes=True), [], ["gx"])
+    op("g", lambda e: e.iota(V("gx", 14, 128, 16), [[-4, 2], [1, 4]], 4, 0, allow_small_or_imprecise_dtypes=True), [], ["gx"])
+    iota("jd", 0, 128, [[1, 8], [0, 16]])
+    iota("ta", 0, 64, [[32, 2], [0, 2], [1, 16]])
+    iota("ta", 64, 128, [[32, 2], [0, 2], [1, 16]])
+    iota("t16", 0, 16, [[16, 16]])
+    iota("jrow", 0, 256, [[1, 256]])
+    iota("ev", 0, 256, [[1, 256]])
+    iota("gc", 0, 128, [[0, 2], [1, 2], [0, 32]])
+    iota("coff", 0, 64, [[1024, 4], [1, 16]])
+    iota("vlf", 0, 8, [[0, 2], [1, 2], [8, 2]])
+    iota("vr", 0, 64, [[0, 16], [1, 2], [0, 2]], 0)
+    iota("vr", 64, 128, [[0, 16], [1, 2], [0, 2]], 2)
+    for a in range(4):
+        for h in range(2):
+            iota("wlf", 32 * a + h, 32 * a + 32, [[128, 4], [0, 2], [32, 2]], 64 * (a >> 1) + 16 * (a & 1), 0, 2)
+
+    def bits(j, sh, m):
+        op("v", lambda e: e.tensor_scalar(V("ci", j, j + 1), V("ci", 0, 1), sh, m, A.logical_shift_right, A.bitwise_and), ["ci"], ["ci." + str(j)], True)
+    for j, sh, m in ((1, 0, 15), (2, 4, 7), (3, 4, 1), (4, 6, 1), (5, 5, 1), (6, 5, 1), (7, 0, 15), (8, 0, 1), (9, 2, 3)):
+        bits(j, sh, m)
+    ci_all = ["ci"] + ["ci." + str(j) for j in range(1, 10)]
+    vc(V("cf", 0, 10), V("ci", 0, 10), ci_all, ["cf"])
+
+    def cf(j):
+        return V("cf", j, j + 1)
+
+    def cs_(j, i, s1, o0, s2=None, o1=None, rd=()):
+        ts(cf(j), cf(i), s1, o0, s2, o1, ["cf"] + list(rd), ["cf.%d" % j])
+
+    ts(V("oh", 0, 16), V("jm", 0, 16), cf(1), A.is_equal, None, None, ["jm", "cf"], ["oh"])
+    ts(V("mask", 0, 256), V("jm", 0, 256), cf(1), A.is_equal, None, None, ["jm", "cf"], ["mask"])
+    ts(V("rst", 0, 256), V("jm", 0, 256), 0.5, A.is_ge, None, None, ["jm"], ["rst"])
+    ts(V("pen", 0, 256), V("jm", 0, 256), cf(1), A.is_gt, 1e29, A.mult, ["jm", "cf"], ["pen"])
+    vc(V("ul", 0, 24), V("ulf", 0, 24), ["ulf"], ["ul"])
+    ts(V("l15", 0, 16), V("t16", 0, 16), 15.0, A.add, None, None, ["t16"], ["l15"])
+    ts(V("ql", 0, 8), V("jm", 0, 8), 0.0, A.mult, cf(1), A.add, ["jm", "cf"], ["ql"])
+    quant("uq", "us", 0, 128, "ut", ["ut"], ["uq"])
+    op("v", lambda e: e.tensor_copy(V("up", 0, 384).bitcast(dt.uint32), V("uq", 0, 128).bitcast(dt.uint32).indirect(V("ul", 0, 24))), ["uq", "ul"], ["up"])
+    op("a", lambda e: e.activation(V("ups", 0, 384), ind("us", 0, 128, "ul", 0, 24), AF.Copy), ["uq", "ul"], ["ups"])
+    quant("xq", "xs", 0, 256, "xt", ["xt"], ["xq"])
+    zero("dtl", [], lanes("dtl"))
+
+    def scores():
+        for bank, c in ((0, 0), (6, 0), (4, 1), (5, 2)):
+            mm(bank, 256, "up", "ups", 128 * c, "xq", "xs", 0, True, True, ["up", "ups", "xq"])
+        for bank, n in ((6, "sw0"), (4, "sw1"), (5, "sw2")):
+            act(V(n, 0, 256), V("pb%d" % bank, 0, 256), ["pb%d" % bank], [n])
+
+    def far_scores():
+        for k in range(3):
+            act(V("n%d" % k, 0, 256), ind("sw%d" % k, 0, 256, "lku", 16 * k, 16 * k + 16), ["sw%d" % k, "lku"], ["n%d" % k])
+
+    def setup_late():
+        oh = lambda a, b: V("oh", a, b)
+        cs_(28, 3, 256.0, A.mult)
+        cs_(29, 3, -256.0, A.mult, 256.0, A.add)
+        cs_(30, 28, 512.0, A.add, rd=["cf.28"])
+        cs_(6, 4, 512.0, A.mult, cf(28), A.add, ["cf.28"])
+        cs_(7, 4, 512.0, A.mult, cf(29), A.add, ["cf.29"])
+        cs_(8 + 24, 4, -512.0, A.mult, cf(30), A.add, ["cf.30"])
+        cs_(33, 6, -16.0, A.add, rd=["cf.6"])
+        cs_(34, 5, 512.0, A.mult)
+        cs_(26, 1, 64.0, A.mult)
+        cs_(27, 6, 1.0 / 256.0, A.mult, rd=["cf.6"])
+        cs_(35, 8, 16.0, A.mult)
+        cs_(36, 9, 2.0, A.mult, cf(35), A.add, ["cf.35"])
+        for a in range(4):
+            cs_(15 + a, 0, -float(64 * (a >> 1) + 16 * (a & 1)), A.add)
+        vc(V("lku", 0, 48), V("lki", 0, 48), ["lki"], ["lku"])
+        vc(V("lkf", 0, 48), V("lki", 0, 48), ["lki"], ["lkf"])
+        ts(V("m0", 0, 16), V("t16", 0, 16), cf(1), A.add, cf(6), A.add, ["t16", "cf", "cf.6"], ["m0"])
+        for k, j in ((0, 6), (1, 7), (2, 32)):
+            ts(V("lkx", 16 * k, 16 * k + 16), V("lkf", 16 * k, 16 * k + 16), cf(j), A.add, None, None, ["lkf", "cf.%d" % j], ["lkx"], True)
+        ts(V("lkx", 48, 64), V("t16", 0, 16), cf(1), A.add, cf(6), A.add, ["t16", "cf", "cf.6"], ["lkx"], True)
+        tt(V("lt0", 0, 256), ind("jrow", 0, 256, "lku", 0, 16), V("ev", 0, 256), A.is_lt, ["jrow", "ev", "lku"], ["lt0"])
+        vc(V("ci", 10, 11), V("ci", 5, 6), ["ci.5"], ["ci.10"])
+        ts(V("ci", 11, 12), V("ci", 5, 6), 2.0, A.add, None, None, ["ci.5"], ["ci.11"])
+        dma("s", lambda e: e.dma_start(T.tbl[:], T.lkx[:]), ["lkx"], ["tbl"])
+        for h in range(2):
+            dma("g", lambda e: e.indirect_dma_start(V("l4", 2048 * h, 2048 * h + 2048), None, T.tbl[:], IndirectOffsetOnAxis(ap=V("ci", 10 + h, 11 + h), axis=0), bounds_check=3),
+                ["tbl", "ci.%d" % (10 + h)], ["l4.%d" % h])
+        for j, a in ((19, 0), (20, 4), (21, 8), (31, 12)):
+            op("v", lambda e: e.tensor_reduce(cf(j), oh(a, a + 3), AxisListType.X, A.add), ["oh"], ["cf.%d" % j], True)
+        c = lambda *js: ["cf.%d" % j for j in js]
+        cs_(22, 21, cf(31), A.add, oh(3, 4), A.add, c(21, 31) + ["oh"])
+        cs_(37, 22, -0.5, A.add, rd=c(22))
+        op("v", lambda e: e.tensor_scalar(cf(11), oh(7, 8), -2.0, cf(37), A.mult, A.add), ["oh"] + c(37), c(11))
+        op("v", lambda e: e.tensor_scalar(cf(12), oh(11, 12), -1e4, 1e4, A.mult, A.add), ["oh"], c(12))
+        cs_(38, 22, oh(7, 8), A.add, 80.5, A.mult, c(22) + ["oh"])
+        cs_(39, 38, -1.0, A.add, rd=c(38))
+        op("v", lambda e: e.tensor_scalar(cf(13), oh(11, 12), -78.5, cf(39), A.mult, A.add), ["oh"] + c(39), c(13))
+        zero("rb", [], ["rb"])
+        tt(V("mm3", 0, 3), oh(0, 3), oh(8, 11), A.add, ["oh"], ["mm3.0"])
+        tt(V("mm3", 4, 7), oh(4, 7), oh(8, 11), A.add, ["oh"], ["mm3.1"])
+        tt(cf(40), oh(3, 4), oh(7, 8), A.add, ["oh"], c(40))
+        cs_(41, 19, 8.0, A.mult, cf(20), A.subtract, c(19, 20))
+        cs_(42, 21, 7.0, A.mult, cf(41), A.add, c(21, 41))
+        op("v", lambda e: e.tensor_scalar(cf(43), oh(11, 12), 8.0, cf(42), A.mult, A.add), ["oh"] + c(42), c(43))
+        R = lambda a, b, st=1: V("rb", a, b, st)
+
+        def put(out, in0, s1, o0, s2=None, o1=None, rd=()):
+            ts(out, in0, s1, o0, s2, o1, ["oh", "rb"] + list(rd), ["rb.x"], True)
+        m3 = V("mm3", 4, 7)
+        put(R(0, 3), V("mm3", 0, 3), -1.0, A.mult, rd=["mm3.0"])
+        for base in (0, 64):
+            put(R(base + 4, base + 7), m3, -1.0, A.mult, cf(40), A.add, ["mm3.1"] + c(40))
+        put(R(8, 11), m3, 3.0, A.mult, cf(43), A.add, ["mm3.1"] + c(43))
+        put(R(12, 15), m3, 3.0, A.mult, cf(43), A.add, ["mm3.1"] + c(43))
+        cs_(44, 19, cf(21), A.add, oh(11, 12), A.add, c(19, 21) + ["oh"])
+        put(R(3, 4), cf(44), 1.0, A.mult, rd=c(44))
+        cs_(45, 20, cf(21), A.add, -1.0, A.mult, c(20, 21))
+        cs_(46, 40, 3.0, A.mult, cf(45), A.add, c(40, 45))
+        put(R(7, 8), oh(11, 12), 8.0, A.mult, cf(46), A.add, c(46))
+        put(R(11, 12), oh(11, 12), -1.0, A.mult)
+        put(R(64, 67), V("mm3", 0, 3), -1.0, A.mult, oh(11, 12), A.add, ["mm3.0"])
+        put(R(72, 75), V("mm3", 0, 3), -1.0, A.mult, rd=["mm3.0"])
+        put(R(128, 131), oh(8, 11), -1.0, A.mult)
+        put(R(132, 135), oh(4, 7), -1.0, A.mult)
+        cs_(47, 21, 8.0, A.mult, cf(20), A.subtract, c(20, 21))
+        put(R(136, 139), oh(4, 7), 3.0, A.mult, cf(47), A.add, c(47))
+        put(R(140, 143), oh(4, 7), 3.0, A.mult, cf(47), A.add, c(47))
+        put(R(131, 132), cf(21), 1.0, A.mult, rd=c(21))
+        put(R(135, 136), cf(20), -1.0, A.mult, rd=c(20))
+        far = oh(12, 15)
+        for j in (8, 9, 10, 12, 13, 14):
+            for base in (0, 128):
+                put(R(base + 16 + j, base + 64, 16), far, -9.0 if base == 0 else 8.0, A.mult)
+        for base, j, w in ((0, 3, -1.0), (0, 7, -1.0), (128, 3, 1.0)):
+            put(R(base + 16 + j, base + 64, 16), far, w, A.mult)
+        for base, j, w in ((0, 0, 1.0), (0, 4, -1.0), (64, 0, 1.0), (64, 4, -1.0), (64, 8, 1.0), (128, 0, -1.0)):
+            put(R(base + 16 + j, base + 64, 17), far, w, A.mult)
+        for j in (8, 12):
+            ts(R(16 + j, 64, 17), far, -6.0, A.mult, None, None, ["oh", "rb", "rb.x"], ["rb.x"])
+        ts(V("blkx", 0, 128), V("gx", 0, 128), cf(2), A.is_equal, None, None, ["gx", "cf"], ["blkx"])
+        ts(V("kc", 0, 128), V("gx", 0, 128), cf(2), A.is_equal, None, None, ["gx", "cf"], ["kc"])
+        ts(V("kc", 11, 128, 16), V("gx", 11, 128, 16), cf(2), A.is_equal, -1.0, A.mult, ["gx", "cf"], ["kc"])
+        ts(V("kp", 0, 128), V("jd", 0, 128), cf(2), A.is_equal, None, None, ["jd", "cf"], ["kp"])
+        zero("kt", [], ["kt"])
+        for b in range(4):
+            act(V("kt", b, 512, 4), V("kc", 0, 128), ["kc", "kt"], ["kt.o%d" % b])
+            act(V("kt", 512 + b, 1024, 4), V("kp", 0, 128), ["kp", "kt"], ["kt.p%d" % b])
+        names = []
+        for i, m in enumerate(("s", "fin", "init")):
+            o = 4 * K[m]
+            for b in range(4):
+                names.append("kt.%s%d" % (m, b))
+                tt(V("kt", o + b, o + 512, 4), ind("rb", 64 * i + 16 * b, 64 * i + 16 * b + 16, "ql", 0, 8), V("blkx", 0, 128), A.mult, ["rb.x", "ql", "blkx", "kt"], [names[-1]])
+        o = 4 * K["kw"]
+        ts(V("vm", 0, 128), V("gc", 0, 128), cf(5), A.is_equal, 16.0, A.mult, ["gc", "cf"], ["vm.t"])
+        tt(V("kt", o, o + 512, 4), V("vm", 0, 128), V("mask", 0, 128), A.mult, ["vm.t", "mask", "kt"], ["kt.w0"])
+        ts(V("kt", o + 2, o + 512, 4), V("kt", o, o + 512, 4), 2.0, A.mult, None, None, ["kt.w0"], ["kt.w2"])
+        ts(V("vm", 0, 128), V("vr", 0, 128), cf(27), A.is_equal, None, None, ["vr", "cf.27"], ["vm", "vm.t"])
+        put_nd = [(8, 1.0), (9, 2.0), (10, 4.0), (4, 8.0), (5, 16.0), (6, 32.0)]
+        prev = None
+        for i, (q, w) in enumerate(put_nd):
+            j = 50 + i % 2
+            if prev is None:
+                op("v", lambda e: e.tensor_scalar(cf(j), oh(q, q + 1), w, None, A.mult), ["oh"], c(j))
+            else:
+                op("v", lambda e: e.tensor_scalar(cf(j), oh(q, q + 1), w, cf(prev), A.mult, A.add), ["oh"] + c(prev), c(j))
+            prev = j
+        o = 4 * K["nd"]
+        ts(V("kt", o, o + 512, 4), V("jd", 0, 128), cf(2), A.is_equal, cf(prev), A.mult, ["jd", "cf", "kt"] + c(prev), ["kt.n0"])
+        kt_all = ["kt"] + names + ["kt.w0", "kt.w2", "kt.n0"] + ["kt.%s%d" % (x, b) for x in "op" for b in range(4)]
+        quant("kq", "ks", 0, 512, "kt", kt_all, ["kq"])
+        quant("kq", "ks", 512, 896, "kt", kt_all, ["kq.2"], 2048)
+        for a in range(4):
+            ts(V("zc", 128 * a, 128 * a + 128), V("ta", 0, 128), cf(15 + a), A.is_equal, 0.5, A.mult, ["ta", "cf.%d" % (15 + a)], ["zc.%d" % a])
+        zero("ke0", [], ["ke0"])
+        zero("ke1", [], ["ke1"])
+        for a in range(4):
+            n = "ke%d" % (a % 2)
+            for b in range(4):
+                act(V(n, 512 * b + b, 512 * b + 512, 4), V("zc", 128 * a, 128 * a + 128), ["zc.%d" % a, n], ["%s.%d" % (n, b)])
+            quant("keq", "kes", 512 * a, 512 * a + 512, n, [n] + lanes(n), ["keq.%d" % a])
+        ts(V("coff", 0, 64), V("coff", 0, 64), cf(26), A.add, None, None, ["coff", "cf.26"], ["coff"])
+        ts(V("vl", 0, 8), V("vlf", 0, 8), cf(36), A.add, None, None, ["vlf", "cf.36"], ["vl"])
+        ts(V("wl", 0, 128), V("wlf", 0, 128), cf(1), A.add, None, None, ["wlf", "cf"], ["wl"])
+        for n in ("ct", "ct2", "cc"):
+            zero(n, [], lanes(n))
+        zero("vt", [], ["vt"])
+        zero("et", [], lanes("et"))
+        quant("zq", "zs", 0, 128, "vt", ["vt"], ["zq"])
+        quant("vq", "vs", 0, 128, "vt0", ["vt0"], ["vq"])
+        for t in range(ROUNDS):
+            dma("s", lambda e: e.dma_start(V("aq%d" % t, GW, 128).bitcast(dt.uint8), V("zq", GW, 128).bitcast(dt.uint8)), ["zq"], ["aq%d" % t])
+            dma("s", lambda e: e.dma_start(V("as%d" % t, GW, 128), V("zs", GW, 128)), ["zq"], ["as%d" % t])
+
+    def layers():
+        op("v", lambda e: e.tensor_copy(V("wp", 0, 2048).bitcast(dt.uint32), V("wq", 0, 512).bitcast(dt.uint32).indirect(V("wl", 0, 128))), ["wq", "wl"], ["wp"])
+        op("a", lambda e: e.activation(V("wps", 0, 2048), ind("wsx", 0, 512, "wl", 0, 128), AF.Copy), ["wsx", "wl"], ["wps"])
+
+    hw_lanes = ["hw.%d.%d" % (b, a) for b in range(4) for a in range(4)]
+
+    def pick(n, off, oa, ob, dst, dst_at, name):
+        rd = ["da.0", "da.1"] if n == "da" else [n + ".0", n + ".1"]
+        tt(V("hp", 0, 256), ind(n, 0, 1024, off, oa, ob), V("mask", 0, 256), A.mult, rd + ["mask", name], ["hp"])
+        op("v", lambda e: e.tensor_tensor_scan(V("hs", 0, 256), V("rst", 0, 256), V("hp", 0, 256), 0.0, A.mult, A.add), ["rst", "hp"], ["hs"])
+        vc(V(dst, dst_at, dst_at + 16), V("hs", 15, 256, 16), ["hs"], [dst + ".%d" % dst_at])
+
+    fw_lanes = ["fw.%d.%d" % (b, a) for b in range(4) for a in range(4)]
+
+    def unpack():
+        i = 0
+        for a in range(4):
+            for b in range(4):
+                bank = 4 + i % 4
+                mm(bank, 256, "keq", "kes", 512 * a + 128 * b, "xq", "xs", 0, True, True, ["keq.%d" % a, "xq"])
+                o = 1024 * b + 256 * a
+                act(V("fw", o, o + 256), V("pb%d" % bank, 0, 256), ["pb%d" % bank], ["fw.%d.%d" % (b, a)])
+                i += 1
+
+    def d_start():
+        ts(V("dh", 0, 256), V("pb2", 0, 256), cf(11), A.is_ge, cf(12), A.mult, ["pb2", "cf.11", "cf.12"], ["dh"])
+        act(V("dh2", 0, 256), V("dh", 0, 256), ["dh", "cf.13"], ["dh2"], bias=cf(13))
+
+    dst = T.cores[(rank + 1) % N]
+    via = helper_of(topo, core, dst)
+
+    for t in range(ROUNDS):
+        last = t == ROUNDS - 1
+        scores()
+        if t == 0:
+            setup_late()
+            far_scores()
+        else:
+            mm(2, 256, "kq", "ks", K["init"], "ccq", "ccs", 0, True, True, ["kq", "ccq"])
+            d_start()
+        unpack()
+        if t:
+            far_scores()
+        tt(V("so", 0, 256), V("pb0", 0, 256), V("mask", 0, 256), A.mult, ["pb0", "mask"], ["so"])
+        op("v", lambda e: e.tensor_tensor_scan(V("wsc", 0, 256), V("rst", 0, 256), V("so", 0, 256), 0.0, A.mult, A.add), ["rst", "so"], ["wsc"])
+        tt(V("wm", 0, 256), ind("wsc", 0, 256, "l15", 0, 16), V("pen", 0, 256), A.add, ["wsc", "l15", "pen"], ["wm"])
+        tt(V("dtl", 0, 1024, 4), V("pb0", 0, 256), V("wm", 0, 256), A.not_equal, ["pb0", "wm"], ["dtl.0"])
+        quant("cq", "cs", 1024, 1280, "dtl", lanes("dtl"), ["cq.4"])
+        kinds = (("own", 1), ("pl", 3))
+        for m, bank in kinds:
+            mm(bank, 256, "kq", "ks", K[m], "cq", "cs", 1024, True, False, ["kq", "cq.4"])
+        for tile in range(4):
+            n = "cm%d" % (tile % 2)
+            for el in range(4):
+                c = 4 * tile + el
+                sc = V("wsc", 16 * c + 15, 16 * c + 16)
+                if c:
+                    ts(V(n, el, 64 * c, 4), V("pb0", 0, 16 * c), sc, A.is_gt, None, None, ["pb0", "wsc"], ["%s.%dl" % (n, el)])
+                ts(V(n, 64 * c + el, 1024, 4), V("pb0", 16 * c, 256), sc, A.is_ge, None, None, ["pb0", "wsc"], ["%s.%dr" % (n, el)])
+            quant("cq", "cs", 256 * tile, 256 * tile + 256, n, ["%s.%d%s" % (n, el, s) for el in range(4) for s in "lr"], ["cq.%d" % tile])
+            for m, bank in kinds:
+                mm(bank, 256, "kq", "ks", K[m], "cq", "cs", 256 * tile, False, tile == 3, ["kq", "cq.%d" % tile])
+            if t == 0 and tile == 2:
+                for k in range(3):
+                    nk = V("n%d" % k, 0, 256)
+                    tt(V("ct", 1 + k, 1024, 4), nk, V("pb0", 0, 256), A.is_lt, ["pb0", "n%d" % k], lanes("ct", 1 + k))
+                    tt(V("ct2", 1 + k, 1024, 4), nk, V("pb0", 0, 256), A.is_equal, ["pb0", "n%d" % k], lanes("ct2", 1 + k))
+                l = V("ct2", 1, 1024, 4)
+                tt(V("r1", 0, 256), l, V("lt0", 0, 256), A.mult, lanes("ct2", 1) + ["lt0"], ["r1"])
+                vc(l, V("r1", 0, 256), ["r1"], lanes("ct2", 1))
+                for k, j in ((1, 3), (2, 4)):
+                    l2 = V("ct2", 1 + k, 1024, 4)
+                    ts(l2, l2, cf(j), A.mult, None, None, lanes("ct2", 1 + k) + ["cf"], lanes("ct2", 1 + k))
+                for i, n2 in enumerate(("ct", "ct2")):
+                    quant("ctq", "cts", 256 * i, 256 * i + 256, n2, lanes(n2), ["ctq.%d" % i])
+                    mm(2, 256, "kq", "ks", K["init"], "ctq", "cts", 256 * i, i == 0, i == 1, ["kq", "ctq.%d" % i])
+                d_start()
+        tt(V("bw", 0, 256), V("pb1", 0, 256), V("dh2", 0, 256), A.is_gt, ["pb1", "dh2"], ["bw"])
+
+        def fill_wrap():
+            act(V("rr", 0, 256), V("pb3", 0, 256), ["pb3", "cf.33"], ["rr"], bias=cf(33))
+            tt(V("r1", 0, 256), V("pb3", 0, 256), V("mask", 0, 256), A.mult, ["pb3", "mask"], ["r1"])
+            op("v", lambda e: e.tensor_tensor_scan(V("r2", 0, 256), V("rst", 0, 256), V("r1", 0, 256), 0.0, A.mult, A.add), ["rst", "r1"], ["r2"])
+            ts(V("mu", 96, 112), V("r2", 15, 256, 16), -16.0, A.add, None, None, ["r2"], ["mu.96"])
+
+        def fill_places():
+            dma("s", lambda e: e.dma_start(T.tbh[:], T.rr[0:128:16, :]), ["rr"], ["tbh"])
+            for h in range(2):
+                dma("g", lambda e: e.indirect_dma_start(V("ho", 512 * h, 512 * h + 512), None, T.tbh[:], IndirectOffsetOnAxis(ap=V("ci", 10 + h, 11 + h), axis=0), bounds_check=3),
+                    ["tbh", "ci.%d" % (10 + h)], ["ho.%d" % h])
+            op("v", lambda e: e.tensor_copy(V("lw", 0, 256).indirect(V("mu", 96, 112)), V("jrow", 0, 256)), ["mu.96", "jrow"], ["lw"])
+
+        def fill_gate():
+            tt(V("r1", 0, 64), V("lw", 0, 64), V("mask", 0, 64), A.mult, ["lw", "mask"], ["r1"])
+            op("v", lambda e: e.tensor_tensor_scan(V("r2", 0, 64), V("rst", 0, 64), V("r1", 0, 64), 0.0, A.mult, A.add), ["rst", "r1"], ["r2"])
+            ts(V("mu", 112, 116), V("r2", 15, 64, 16), cf(6), A.add, None, None, ["r2", "cf.6"], ["mu.112"])
+            for b in range(4):
+                act(V("et", b, 256, 4), ind("fw", 1024 * b, 1024 * b + 1024, "mu", 112, 116), fw_lanes + ["mu.112"], lanes("et", b), scale=2.0)
+
+        def fill_send():
+            quant("eq%d" % t, "es%d" % t, 0, 128, "et", lanes("et"), ["eq%d" % t])
+            waits("g", ["eq%d" % t], [])
+            to = dst if via is None else via
+            p = "a" if via is None else "r"
+            send(g, T, topo, core, to, V("%sq%d" % (p, t), 0, GW), V("eq%d" % t, 0, GW), V("%ss%d" % (p, t), 0, GW), V("es%d" % t, 0, GW),
+                 T.sem["%s%d" % ("arr" if via is None else "rel", t)])
+
+        def fill_turn():
+            for k in range(3):
+                op("v", lambda e: e.transpose(V("nt%d" % k, 0, 256), V("n%d" % k, 0, 256)), ["n%d" % k], ["nt%d" % k])
+
+        def fill_pref():
+            nt = [V("nt%d" % k, 0, 256, 16) for k in range(3)]
+            P = lambda i: V("pw", 16 * i, 16 * i + 16)
+            for i, (x, y) in enumerate(((0, 1), (0, 2), (1, 2))):
+                tt(P(3 + i), nt[x], nt[y], A.is_le, ["nt%d" % x, "nt%d" % y], ["pw.%d" % (3 + i)])
+            tt(P(0), P(3), P(4), A.add, ["pw.3", "pw.4"], ["pw.0"])
+            tt(P(1), P(5), P(3), A.subtract, ["pw.5", "pw.3"], ["pw.1"])
+            tt(P(2), P(4), P(5), A.add, ["pw.4", "pw.5"], ["pw.2"])
+            ts(P(0), P(0), 1.0, A.add, None, None, ["pw.0"], ["pw.0"])
+            ts(P(1), P(1), 2.0, A.add, None, None, ["pw.1"], ["pw.1"])
+            ts(P(2), P(2), -1.0, A.mult, 3.0, A.add, ["pw.2"], ["pw.2"])
+        fills = [fill_wrap, fill_places, fill_gate, fill_send, fill_turn, fill_pref]
+
+        for i in range(SWEEPS):
+            vc(V("st", 0, 1024, 4), V("bw", 0, 256), ["bw"], lanes("st", 0))
+            for k in (1, 2):
+                act(V("st", 1 + k, 1024, 4), ind("bw", 0, 256, "lku", 16 * k, 16 * k + 16), ["bw", "lku"], lanes("st", 1 + k))
+            vc(V("st", 1, 1024, 4), ind("bw", 0, 256, "lku", 0, 16), ["bw", "lku"], lanes("st", 1))
+            quant("sq", "ss", 0, 256, "st", lanes("st"), ["sq"])
+            m = "fin" if i == SWEEPS - 1 else "s"
+            mm(2, 256, "kq", "ks", K[m], "sq", "ss", 0, True, True, ["kq", "kq.2", "sq"])
+            if i < len(fills):
+                fills[i]()
+            if t == 0 and i == 3:
+                layers()
+                zero("hw", [], hw_lanes)
+            ts(V("bw", 0, 256), V("pb2", 0, 256), cf(11) if m == "s" else -0.5, A.is_lt, None, None, ["pb2", "cf.11"], ["bw"])
+        op("v", lambda e: e.transpose(V("bt", 0, 256), V("bw", 0, 256)), ["bw"], ["bt"])
+        tk = lambda i: V("tk", 16 * i, 16 * i + 16)
+        for k in range(3):
+            tt(tk(k), V("bt", k, 256, 16), V("pw", 16 * k, 16 * k + 16), A.mult, ["bt", "pw.%d" % k], ["tk.%d" % k])
+        tt(tk(3), tk(0), tk(1), A.max, ["tk.0", "tk.1"], ["tk.3"])
+        tt(tk(4), tk(3), tk(2), A.max, ["tk.3", "tk.2"], ["tk.4"])
+        for i in range(2):
+            tt(V("eqk", 16 * i, 16 * i + 16), tk(1 + i), tk(4), A.is_equal, ["tk.%d" % (1 + i), "tk.4"], ["eqk.%d" % i])
+        tt(V("vt", 0, 256, 2), ind("eqk", 0, 32, "vl", 0, 8), V("vm", 0, 128), A.mult, ["eqk.0", "eqk.1", "vl", "vm"], ["vt"])
+        quant("vtq", "vts", 0, 128, "vt", ["vt"], ["vtq"])
+        mm(0, 128, "kq", "ks", K["kw"], "vtq", "vts", 0, True, True, ["kq.2", "vtq"])
+        tt(V("of", 0, 64), V("pb0", 0, 64), V("coff", 0, 64), A.add, ["pb0", "coff"], ["of"])
+        vc(V("ou", 0, 64), V("of", 0, 64), ["of"], ["ou"])
+        l4 = ["l4.0", "l4.1"]
+        op("a", lambda e: e.activation(V("da", 512, 1024), ind("l4", 0, 4096, "ou", 32, 64), AF.Copy), l4 + ["ou"], ["da.1"])
+        vc(V("da", 0, 512), ind("l4", 0, 4096, "ou", 0, 32), l4 + ["ou"], ["da.0"])
+        if True:
+            Q["t"].wait_ge(T.sem["arr%d" % t], 2 * NE)
+        pick("da", "m0", 0, 16, "mu", 0, "m0")
+        for b in range(4):
+            act(V("fd", 256 * b, 256 * b + 256), ind("fw", 1024 * b, 1024 * b + 1024, "mu", 0, 16), fw_lanes + ["mu.0"], ["fd.%d" % b])
+        i = 0
+        for a in range(4):
+            for b in range(4):
+                bank = 4 + i % 4
+                mm(bank, 128, "wp", "wps", 512 * a + 128 * b, "aq%d" % t, "as%d" % t, 0, True, True, ["wp", "wps", "aq%d" % t, "as%d" % t])
+                o = 1024 * b + 256 * a
+                act(V("hw", o, o + GW), V("pb%d" % bank, 0, GW), ["pb%d" % bank], ["hw.%d.%d" % (b, a)], scale=0.015625)
+                i += 1
+        pick("da", "mu", 0, 16, "mu", 16, "mu.0")
+        pick("da", "mu", 16, 32, "mu", 32, "mu.16")
+        pick("da", "mu", 32, 48, "mu", 48, "mu.32")
+        pick("ho", "mu", 48, 64, "mu", 64, "mu.48")
+        for b in range(4):
+            tt(V("zb", 256 * b, 256 * b + 256), ind("fw", 1024 * b, 1024 * b + 1024, "mu", 48, 64), V("fd", 256 * b, 256 * b + 256), A.add,
+               fw_lanes + ["mu.48", "fd.%d" % b], ["zb.%d" % b])
+        for b in range(4):
+            tt(V("xn", b, 1024, 4), ind("hw", 1024 * b, 1024 * b + 1024, "mu", 64, 80), V("zb", 256 * b, 256 * b + 256), A.add,
+               hw_lanes + ["mu.64", "zb.%d" % b], lanes("xn", b))
+        quant("xq", "xs", 0, 256, "xn", lanes("xn"), ["xq"])
+        vc(V("cc", 0, 1024, 4), V("bw", 0, 256), ["bw"], lanes("cc", 0))
+        quant("ccq", "ccs", 0, 256, "cc", lanes("cc"), ["ccq"])
+        if last:
+            dma("s", lambda e: e.dma_start(T.oc[:, :], T.xq[:].bitcast(dt.uint8)), ["xq"], ["out.oc"])
+            for k in range(4):
+                dma("s", lambda e: e.dma_start(T.osc[4 * k:4 * k + 4, :], T.xs[32 * k:32 * k + 4, :]), ["xq"], ["out.os%d" % k])
+            mm(4, 256, "vq", "vs", 0, "xq", "xs", 0, True, True, ["vq", "xq"])
+            mm(5, 256, "kq", "ks", K["nd"], "ccq", "ccs", 0, True, True, ["kq.2", "ccq"])
+            act(V("ev", 0, 256), ind("da", 0, 1024, "mu", 32, 48), ["da.0", "da.1", "mu.32"], ["ev.0"])
+            act(V("ys", 0, 256), V("pb4", 0, 256), ["pb4"], ["ys"])
+            dma("s", lambda e: e.dma_start(T.y[:, :], T.ys[:]), ["ys"], ["out.y"])
+            act(V("ndb", 256, 512), V("pb5", 0, 256), ["pb5"], ["ndb.1"])
+            ts(V("ev", 256, 512), V("ev", 0, 256), 512.0, A.is_ge, 512.0, A.mult, ["ev.0"], ["ev.1"])
+            ts(V("hp", 0, 256), V("ev", 0, 256), cf(34), A.add, None, None, ["ev.0", "cf.34"], ["hp"])
+            tt(V("ndb", 0, 256), V("hp", 0, 256), V("ev", 256, 512), A.add, ["hp", "ev.1"], ["ndb.0"])
+            dma("s", lambda e: e.dma_start(T.nd[:, :], T.ndb[0:128:16, :]), ["ndb.0", "ndb.1"], ["out.nd"])
+    for s in sorted(cnt):
+        if known["g"].get(s, 0) < cnt[s]:
+            g.wait_ge(T.sem[s], cnt[s])
+    g.wait_ge(T.sem.loc, 2 * NE * ROUNDS)

@@ -11,18 +11,18 @@ SCRATCH = {
     "up": ("sbuf", [128, 384], F8), "ups": ("sbuf", [128, 384], U8), "vq": ("sbuf", [128, 128], F8), "vs": ("sbuf", [128, 128], U8),
     "wq": ("sbuf", [128, 512], F8), "wsx": ("sbuf", [128, 512], U8), "wp": ("sbuf", [128, 2048], F8), "wps": ("sbuf", [128, 2048], U8),
     "ci": ("sbuf", [128, 16], I32), "cf": ("sbuf", [128, 64], F32), "jm": ("sbuf", [128, 256], F32), "jd": ("sbuf", [128, 128], F32),
-    "jrow": ("sbuf", [128, 256], F32), "gx": ("sbuf", [128, 128], F32), "gc": ("sbuf", [128, 128], F32), "ta": ("sbuf", [128, 128], F32),
+    "jrow": ("sbuf", [128, 256], F32), "gx": ("sbuf", [128, 128], F32), "gc": ("sbuf", [128, 128], F32), "half": ("sbuf", [128, 64], BF), "z0": ("sbuf", [128, 1024], BF), "qlf": ("sbuf", [128, 32], F32), "bx4": ("sbuf", [128, 512], F32),
     "ulf": ("sbuf", [128, 24], F32), "ul": ("sbuf", [128, 24], U16), "wlf": ("sbuf", [128, 128], F32), "wl": ("sbuf", [128, 128], U16),
-    "t16": ("sbuf", [128, 16], F32), "l15": ("sbuf", [128, 16], U16), "m0": ("sbuf", [128, 16], U16), "ql": ("sbuf", [128, 8], U16),
+    "t16": ("sbuf", [128, 16], F32), "l15": ("sbuf", [128, 16], U16), "m0": ("sbuf", [128, 16], U16), "ql": ("sbuf", [128, 32], U16),
     "coff": ("sbuf", [128, 64], F32), "vlf": ("sbuf", [128, 8], F32), "vl": ("sbuf", [128, 8], U16), "vr": ("sbuf", [128, 128], F32),
     "vm": ("sbuf", [128, 128], F32), "mask": ("sbuf", [128, 256], F32), "rst": ("sbuf", [128, 256], F32), "pen": ("sbuf", [128, 256], F32),
     "oh": ("sbuf", [128, 16], F32), "rb": ("sbuf", [128, 192], F32), "mm3": ("sbuf", [128, 8], F32), "blkx": ("sbuf", [128, 128], F32),
     "kc": ("sbuf", [128, 128], BF), "kp": ("sbuf", [128, 128], BF), "kt": ("sbuf", [128, 3584], BF), "kq": ("sbuf", [128, 896], F8), "ks": ("sbuf", [128, 896], U8),
-    "zc": ("sbuf", [128, 512], BF), "ke0": ("sbuf", [128, 2048], BF), "ke1": ("sbuf", [128, 2048], BF),
+    "ke0": ("sbuf", [128, 2048], BF), "ke1": ("sbuf", [128, 2048], BF),
     "keq": ("sbuf", [128, 2048], F8), "kes": ("sbuf", [128, 2048], U8), "lt0": ("sbuf", [128, 256], F32),
     "sw": ("sbuf", [128, 768], F32), "nn": ("sbuf", [128, 768], F32), "nt": ("sbuf", [128, 768], F32), "pw": ("sbuf", [128, 96], F32),
     "so": ("sbuf", [128, 256], F32), "wsc": ("sbuf", [128, 256], F32), "wm": ("sbuf", [128, 256], F32), "dtl": ("sbuf", [128, 1024], BF),
-    "cm0": ("sbuf", [128, 1024], BF), "cm1": ("sbuf", [128, 1024], BF), "cq": ("sbuf", [128, 1280], F8), "cs": ("sbuf", [128, 1280], U8),
+    "cm0": ("sbuf", [128, 1024], BF), "cm2": ("sbuf", [128, 1024], BF), "sg": ("sbuf", [128, 1024], BF), "cm1": ("sbuf", [128, 1024], BF), "cq": ("sbuf", [128, 1280], F8), "cs": ("sbuf", [128, 1280], U8),
     "ct": ("sbuf", [128, 1024], BF), "ct2": ("sbuf", [128, 1024], BF), "cc": ("sbuf", [128, 1024], BF), "ctq": ("sbuf", [128, 512], F8), "cts": ("sbuf", [128, 512], U8),
     "ccq": ("sbuf", [128, 256], F8), "ccs": ("sbuf", [128, 256], U8), "dh": ("sbuf", [128, 256], F32), "dh2": ("sbuf", [128, 256], F32),
     "bw": ("sbuf", [128, 256], BF), "st": ("sbuf", [128, 1024], BF), "sq": ("sbuf", [128, 256], F8), "ss": ("sbuf", [128, 256], U8),
@@ -42,7 +42,8 @@ PIECE = {}
 for _n, _w, _k in (("pb", 512, 8), ("sw", 256, 3), ("n", 256, 3), ("nt", 256, 3), ("eq", 128, 3), ("es", 128, 3), ("rq", GW, 3), ("rs", GW, 3), ("aq", 128, 3), ("as", 128, 3)):
     for _i in range(_k):
         PIECE["%s%d" % (_n, _i)] = ("nn" if _n == "n" else _n, _w * _i)
-SEMAPHORES = ["qv", "qa", "qt", "qp", "loc"] + ["arr%d" % i for i in range(ROUNDS)] + ["rel%d" % i for i in range(ROUNDS)] + ["d%d" % i for i in range(48)]
+SEMAPHORES = ["qv", "qa", "qt", "qp", "loc"] + ["arr%d" % i for i in range(ROUNDS)] + ["rel%d" % i for i in range(ROUNDS)] + ["d%d" % i for i in range(64)]
+EXTRA, SOME = 1, (2, 3, 3, 3)
 NE = 4
 
 
@@ -194,6 +195,12 @@ def rank_program(g, core, T, topo):
         op("t", lambda e: e.matmul_mx(V("pb%d" % bank, 0, n), V(lq, la, la + 128), V(ls, la, la + 128), V(rq, ra, ra + n), V(rs, ra, ra + n), start, stop),
            rd, ["pb%d" % bank])
 
+    def clear(n, w, wr):
+        for a in range(0, w, 1024):
+            k = min(1024, w - a)
+            dma("s", lambda e: e.dma_start(V(n, a, a + k), V("z0", 0, k)), ["z0"], [wr + "/%d" % a])
+        return [wr + "/%d" % a for a in range(0, w, 1024)]
+
     def ind(n, a, b, off, oa, ob):
         return V(n, a, b).indirect(V(off, oa, ob))
 
@@ -206,8 +213,30 @@ def rank_program(g, core, T, topo):
     dma("s", lambda e: e.dma_start(T.wsx[:], T.ws[:, :]), [], ["wsx"])
     dma("s", lambda e: e.dma_start(T.vt0[:], T.v[:, :]), [], ["vt0"])
 
+    zero("z0", [], ["z0"])
+    z_ke = [clear("ke0", 2048, "z.ke0"), clear("ke1", 2048, "z.ke1")]
+    zero("rb", [], ["rb"])
+    op("v", lambda e: e.memset(T.half[:], 0.5), [], ["half"])
+    for j, w in ((56, -0.5), (57, 0.5), (58, 1.0), (59, 2.0), (60, 3.0)):
+        op("v", lambda e: e.memset(V("cf", j, j + 1), w), [], ["cf.%d" % j])
+    for n in ("dtl", "ct", "ct2", "cc"):
+        z = clear(n, 1024, "z." + n)
+        for l in lanes(n):
+            wrote[l] = wrote[z[0]]
+    dma("a", lambda e: e.dma_start(V("kt", 2560, 3584), V("z0", 0, 1024)), ["z0"], ["z.kt"])
+    z_kt = ["z.kt"]
+    for n in ("vt", "et"):
+        z = clear(n, 512, "z." + n)
+        for l in lanes(n) + [n]:
+            wrote[l] = wrote[z[0]]
+    z_hw = clear("hw", 4096, "z.hw")
+    for b in range(4):
+        for a in range(4):
+            wrote["hw.%d.%d" % (b, a)] = wrote[z_hw[b]]
+
     iota("ci", 0, 1, [[0, 1]], 0, 1)
     iota("jm", 0, 256, [[0, 16], [1, 16]])
+    iota("qlf", 0, 32, [[0, 8], [4, 4]])
     iota("ulf", 0, 8, [[16, 8]])
     iota("ulf", 8, 16, [[32, 4], [-16, 2]], 16)
     iota("ulf", 16, 24, [[-64, 2], [16, 4]], 64)
@@ -215,8 +244,6 @@ def rank_program(g, core, T, topo):
     op("g", lambda e: e.iota(V("gx", 13, 128, 16), [[2, 4], [-1, 2]], 1, 0, allow_small_or_imprecise_dtypes=True), [], ["gx"])
     op("g", lambda e: e.iota(V("gx", 14, 128, 16), [[-4, 2], [1, 4]], 4, 0, allow_small_or_imprecise_dtypes=True), [], ["gx"])
     iota("jd", 0, 128, [[1, 8], [0, 16]])
-    iota("ta", 0, 64, [[32, 2], [0, 2], [1, 16]])
-    iota("ta", 64, 128, [[32, 2], [0, 2], [1, 16]])
     iota("t16", 0, 16, [[16, 16]])
     iota("jrow", 0, 256, [[1, 256]])
     iota("ev", 0, 256, [[1, 256]])
@@ -231,7 +258,7 @@ def rank_program(g, core, T, topo):
 
     def bits(j, sh, m):
         op("v", lambda e: e.tensor_scalar(V("ci", j, j + 1), V("ci", 0, 1), sh, m, A.logical_shift_right, A.bitwise_and), ["ci"], ["ci." + str(j)], True)
-    for j, sh, m in ((1, 0, 15), (2, 4, 7), (3, 4, 1), (4, 6, 1), (5, 5, 1), (6, 5, 1), (7, 0, 15), (8, 0, 1), (9, 2, 3)):
+    for j, sh, m in ((1, 0, 15), (2, 4, 7), (3, 4, 1), (4, 6, 1), (5, 5, 1), (6, 5, 1), (7, 0, 3), (8, 0, 1), (9, 2, 3)):
         bits(j, sh, m)
     ci_all = ["ci"] + ["ci." + str(j) for j in range(1, 10)]
     vc(V("cf", 0, 10), V("ci", 0, 10), ci_all, ["cf"])
@@ -239,8 +266,20 @@ def rank_program(g, core, T, topo):
     def cf(j):
         return V("cf", j, j + 1)
 
+    def lin(out, in0, s1, o0, s2, o1, rd, wr, free=False):
+        if o0 == A.mult and (o1 is None or o1 == A.add):
+            if s2 is None:
+                op("a", lambda e: e.activation(out, in0, AF.Copy, scale=s1), rd, wr, free)
+            else:
+                op("a", lambda e: e.activation(out, in0, AF.Identity, bias=s2, scale=s1), rd, wr, free)
+        elif o0 == A.add and o1 is None:
+            op("a", lambda e: e.activation(out, in0, AF.Identity, bias=s1, scale=1.0), rd, wr, free)
+        else:
+            ts(out, in0, s1, o0, s2, o1, rd, wr, free)
+
     def cs_(j, i, s1, o0, s2=None, o1=None, rd=()):
-        ts(cf(j), cf(i), s1, o0, s2, o1, ["cf"] + list(rd), ["cf.%d" % j])
+        lin(cf(j), cf(i), s1, o0, s2, o1, ["cf"] + list(rd), ["cf.%d" % j])
+
 
     ts(V("oh", 0, 16), V("jm", 0, 16), cf(1), A.is_equal, None, None, ["jm", "cf"], ["oh"])
     ts(V("mask", 0, 256), V("jm", 0, 256), cf(1), A.is_equal, None, None, ["jm", "cf"], ["mask"])
@@ -248,12 +287,33 @@ def rank_program(g, core, T, topo):
     ts(V("pen", 0, 256), V("jm", 0, 256), cf(1), A.is_gt, 1e29, A.mult, ["jm", "cf"], ["pen"])
     vc(V("ul", 0, 24), V("ulf", 0, 24), ["ulf"], ["ul"])
     ts(V("l15", 0, 16), V("t16", 0, 16), 15.0, A.add, None, None, ["t16"], ["l15"])
-    ts(V("ql", 0, 8), V("jm", 0, 8), 0.0, A.mult, cf(1), A.add, ["jm", "cf"], ["ql"])
+    ts(V("blkx", 0, 128), V("gx", 0, 128), cf(2), A.is_equal, None, None, ["gx", "cf"], ["blkx"])
+    ts(V("kc", 0, 128), V("gx", 0, 128), cf(2), A.is_equal, None, None, ["gx", "cf"], ["kc"])
+    ts(V("kc", 11, 128, 16), V("gx", 11, 128, 16), cf(2), A.is_equal, -1.0, A.mult, ["gx", "cf"], ["kc"])
+    ts(V("kp", 0, 128), V("jd", 0, 128), cf(2), A.is_equal, None, None, ["jd", "cf"], ["kp"])
+    vc(V("lku", 0, 48), V("lki", 0, 48), ["lki"], ["lku"])
     quant("uq", "us", 0, 128, "ut", ["ut"], ["uq"])
     op("v", lambda e: e.tensor_copy(V("up", 0, 384).bitcast(dt.uint32), V("uq", 0, 128).bitcast(dt.uint32).indirect(V("ul", 0, 24))), ["uq", "ul"], ["up"])
     op("a", lambda e: e.activation(V("ups", 0, 384), ind("us", 0, 128, "ul", 0, 24), AF.Copy), ["uq", "ul"], ["ups"])
     quant("xq", "xs", 0, 256, "xt", ["xt"], ["xq"])
-    zero("dtl", [], lanes("dtl"))
+    for b in range(4):
+        act(V("kt", b, 512, 4), V("kc", 0, 128), ["kc"], ["kt.o%d" % b])
+        act(V("kt", 512 + b, 1024, 4), V("kp", 0, 128), ["kp"], ["kt.p%d" % b])
+    c55 = []
+
+    def setup_unpack(a):
+        n = "ke%d" % (a % 2)
+        quant("keq", "kes", 512 * a, 512 * a + 512, n, z_ke[a % 2] + lanes(n), ["keq.%d" % a])
+
+    def tiles_unpack(a):
+        n = "ke%d" % (a % 2)
+        for b in range(4):
+            for h in range(2):
+                o = 512 * b + b + 256 * h
+                op("g", lambda e: e.affine_select(V(n, o, 512 * b + 256 * h + 256, 4), V("half", 0, 64), [[-32, 2], [0, 2], [-1, 16]], A.is_equal, 0.0,
+                                                  -(64 * (a >> 1) + 16 * (a & 1)), 1), ["half"] + z_ke[a % 2], ["%s.%d" % (n, b)], True)
+    tiles_unpack(0)
+    tiles_unpack(1)
 
     def scores():
         for bank, c in ((0, 0), (6, 0), (4, 1), (5, 2)):
@@ -267,24 +327,25 @@ def rank_program(g, core, T, topo):
 
     def setup_late():
         oh = lambda a, b: V("oh", a, b)
+        for b in range(4):
+            act(V("bx4", b, 512, 4), V("blkx", 0, 128), ["blkx"], lanes("bx4", b))
+        cs_(49, 7, 16.0, A.mult, cf(9), A.add)
+        ts(V("ql", 0, 32), V("qlf", 0, 32), cf(49), A.add, None, None, ["qlf", "cf.49"], ["ql"])
         cs_(28, 3, 256.0, A.mult)
         cs_(29, 3, -256.0, A.mult, 256.0, A.add)
         cs_(30, 28, 512.0, A.add, rd=["cf.28"])
         cs_(6, 4, 512.0, A.mult, cf(28), A.add, ["cf.28"])
-        cs_(7, 4, 512.0, A.mult, cf(29), A.add, ["cf.29"])
+        cs_(24, 4, 512.0, A.mult, cf(29), A.add, ["cf.29"])
         cs_(8 + 24, 4, -512.0, A.mult, cf(30), A.add, ["cf.30"])
-        cs_(33, 6, -16.0, A.add, rd=["cf.6"])
+        cs_(33, 6, 16.0, A.add, rd=["cf.6"])
         cs_(34, 5, 512.0, A.mult)
         cs_(26, 1, 64.0, A.mult)
         cs_(27, 6, 1.0 / 256.0, A.mult, rd=["cf.6"])
         cs_(35, 8, 16.0, A.mult)
         cs_(36, 9, 2.0, A.mult, cf(35), A.add, ["cf.35"])
-        for a in range(4):
-            cs_(15 + a, 0, -float(64 * (a >> 1) + 16 * (a & 1)), A.add)
-        vc(V("lku", 0, 48), V("lki", 0, 48), ["lki"], ["lku"])
         vc(V("lkf", 0, 48), V("lki", 0, 48), ["lki"], ["lkf"])
         ts(V("m0", 0, 16), V("t16", 0, 16), cf(1), A.add, cf(6), A.add, ["t16", "cf", "cf.6"], ["m0"])
-        for k, j in ((0, 6), (1, 7), (2, 32)):
+        for k, j in ((0, 6), (1, 24), (2, 32)):
             ts(V("lkx", 16 * k, 16 * k + 16), V("lkf", 16 * k, 16 * k + 16), cf(j), A.add, None, None, ["lkf", "cf.%d" % j], ["lkx"], True)
         ts(V("lkx", 48, 64), V("t16", 0, 16), cf(1), A.add, cf(6), A.add, ["t16", "cf", "cf.6"], ["lkx"], True)
         tt(V("lt0", 0, 256), ind("jrow", 0, 256, "lku", 0, 16), V("ev", 0, 256), A.is_lt, ["jrow", "ev", "lku"], ["lt0"])
@@ -299,22 +360,22 @@ def rank_program(g, core, T, topo):
         c = lambda *js: ["cf.%d" % j for j in js]
         cs_(22, 21, cf(31), A.add, oh(3, 4), A.add, c(21, 31) + ["oh"])
         cs_(37, 22, -0.5, A.add, rd=c(22))
-        op("v", lambda e: e.tensor_scalar(cf(11), oh(7, 8), -2.0, cf(37), A.mult, A.add), ["oh"] + c(37), c(11))
-        op("v", lambda e: e.tensor_scalar(cf(12), oh(11, 12), -1e4, 1e4, A.mult, A.add), ["oh"], c(12))
-        cs_(38, 22, oh(7, 8), A.add, 80.5, A.mult, c(22) + ["oh"])
-        cs_(39, 38, -1.0, A.add, rd=c(38))
-        op("v", lambda e: e.tensor_scalar(cf(13), oh(11, 12), -78.5, cf(39), A.mult, A.add), ["oh"] + c(39), c(13))
-        zero("rb", [], ["rb"])
+        lin(cf(11), oh(7, 8), -2.0, A.mult, cf(37), A.add, ["oh"] + c(37), c(11))
+        lin(cf(12), oh(11, 12), -1e4, A.mult, 1e4, A.add, ["oh"], c(12))
+        cs_(38, 22, oh(7, 8), A.add, 295.0, A.mult, c(22) + ["oh"])
+        cs_(39, 38, -200.0, A.add, rd=c(38))
+        lin(cf(13), oh(11, 12), 105.0, A.mult, cf(39), A.add, ["oh"] + c(39), c(13))
         tt(V("mm3", 0, 3), oh(0, 3), oh(8, 11), A.add, ["oh"], ["mm3.0"])
         tt(V("mm3", 4, 7), oh(4, 7), oh(8, 11), A.add, ["oh"], ["mm3.1"])
         tt(cf(40), oh(3, 4), oh(7, 8), A.add, ["oh"], c(40))
-        cs_(41, 19, 8.0, A.mult, cf(20), A.subtract, c(19, 20))
+        cs_(48, 20, -1.0, A.mult, rd=c(20))
+        cs_(41, 19, 8.0, A.mult, cf(48), A.add, c(19, 48))
         cs_(42, 21, 7.0, A.mult, cf(41), A.add, c(21, 41))
-        op("v", lambda e: e.tensor_scalar(cf(43), oh(11, 12), 8.0, cf(42), A.mult, A.add), ["oh"] + c(42), c(43))
+        lin(cf(43), oh(11, 12), 8.0, A.mult, cf(42), A.add, ["oh"] + c(42), c(43))
         R = lambda a, b, st=1: V("rb", a, b, st)
 
         def put(out, in0, s1, o0, s2=None, o1=None, rd=()):
-            ts(out, in0, s1, o0, s2, o1, ["oh", "rb"] + list(rd), ["rb.x"], True)
+            lin(out, in0, s1, o0, s2, o1, ["oh", "rb"] + list(rd), ["rb.x"], True)
         m3 = V("mm3", 4, 7)
         put(R(0, 3), V("mm3", 0, 3), -1.0, A.mult, rd=["mm3.0"])
         for base in (0, 64):
@@ -331,12 +392,15 @@ def rank_program(g, core, T, topo):
         put(R(72, 75), V("mm3", 0, 3), -1.0, A.mult, rd=["mm3.0"])
         put(R(128, 131), oh(8, 11), -1.0, A.mult)
         put(R(132, 135), oh(4, 7), -1.0, A.mult)
-        cs_(47, 21, 8.0, A.mult, cf(20), A.subtract, c(20, 21))
+        cs_(47, 21, 8.0, A.mult, cf(48), A.add, c(21, 48))
         put(R(136, 139), oh(4, 7), 3.0, A.mult, cf(47), A.add, c(47))
         put(R(140, 143), oh(4, 7), 3.0, A.mult, cf(47), A.add, c(47))
         put(R(131, 132), cf(21), 1.0, A.mult, rd=c(21))
         put(R(135, 136), cf(20), -1.0, A.mult, rd=c(20))
         far = oh(12, 15)
+
+        def put(out, in0, s1, o0):
+            ts(out, in0, s1, o0, None, None, ["oh", "rb"], ["rb.v"], True)
         for j in (8, 9, 10, 12, 13, 14):
             for base in (0, 128):
                 put(R(base + 16 + j, base + 64, 16), far, -9.0 if base == 0 else 8.0, A.mult)
@@ -345,57 +409,36 @@ def rank_program(g, core, T, topo):
         for base, j, w in ((0, 0, 1.0), (0, 4, -1.0), (64, 0, 1.0), (64, 4, -1.0), (64, 8, 1.0), (128, 0, -1.0)):
             put(R(base + 16 + j, base + 64, 17), far, w, A.mult)
         for j in (8, 12):
-            ts(R(16 + j, 64, 17), far, -6.0, A.mult, None, None, ["oh", "rb", "rb.x"], ["rb.x"])
-        ts(V("blkx", 0, 128), V("gx", 0, 128), cf(2), A.is_equal, None, None, ["gx", "cf"], ["blkx"])
-        ts(V("kc", 0, 128), V("gx", 0, 128), cf(2), A.is_equal, None, None, ["gx", "cf"], ["kc"])
-        ts(V("kc", 11, 128, 16), V("gx", 11, 128, 16), cf(2), A.is_equal, -1.0, A.mult, ["gx", "cf"], ["kc"])
-        ts(V("kp", 0, 128), V("jd", 0, 128), cf(2), A.is_equal, None, None, ["jd", "cf"], ["kp"])
-        zero("kt", [], ["kt"])
-        for b in range(4):
-            act(V("kt", b, 512, 4), V("kc", 0, 128), ["kc", "kt"], ["kt.o%d" % b])
-            act(V("kt", 512 + b, 1024, 4), V("kp", 0, 128), ["kp", "kt"], ["kt.p%d" % b])
-        names = []
+            ts(R(16 + j, 64, 17), far, -6.0, A.mult, None, None, ["oh", "rb", "rb.v"], ["rb.v"])
+        prev = None
+        for i, (q, w) in enumerate([(8, 1.0), (9, 2.0), (10, 4.0), (4, 8.0), (5, 16.0), (6, 32.0)]):
+            j = 50 + i
+            lin(cf(j), oh(q, q + 1), w, A.mult, cf(prev) if prev else None, A.add if prev else None, ["oh"] + (c(prev) if prev else []), c(j))
+            prev = j
+        c55.append(prev)
+
+    def setup_bits():
         for i, m in enumerate(("s", "fin", "init")):
             o = 4 * K[m]
-            for b in range(4):
-                names.append("kt.%s%d" % (m, b))
-                tt(V("kt", o + b, o + 512, 4), ind("rb", 64 * i + 16 * b, 64 * i + 16 * b + 16, "ql", 0, 8), V("blkx", 0, 128), A.mult, ["rb.x", "ql", "blkx", "kt"], [names[-1]])
+            tt(V("kt", o, o + 512), ind("rb", 64 * i, 64 * i + 64, "ql", 0, 32), V("bx4", 0, 512), A.mult, ["rb.x", "rb.v", "ql"] + lanes("bx4"), ["kt." + m])
+        quant("kq", "ks", 256, 640, "kt", ["kt.s", "kt.fin", "kt.init"], ["kq"], 1024)
+
+    def setup_routes():
+        c = lambda *js: ["cf.%d" % j for j in js]
         o = 4 * K["kw"]
         ts(V("vm", 0, 128), V("gc", 0, 128), cf(5), A.is_equal, 16.0, A.mult, ["gc", "cf"], ["vm.t"])
-        tt(V("kt", o, o + 512, 4), V("vm", 0, 128), V("mask", 0, 128), A.mult, ["vm.t", "mask", "kt"], ["kt.w0"])
-        ts(V("kt", o + 2, o + 512, 4), V("kt", o, o + 512, 4), 2.0, A.mult, None, None, ["kt.w0"], ["kt.w2"])
+        tt(V("kt", o, o + 512, 4), V("vm", 0, 128), V("mask", 0, 128), A.mult, ["vm.t", "mask"] + z_kt, ["kt.w0"])
+        lin(V("kt", o + 2, o + 512, 4), V("kt", o, o + 512, 4), 2.0, A.mult, None, None, ["kt.w0"] + z_kt, ["kt.w2"])
         ts(V("vm", 0, 128), V("vr", 0, 128), cf(27), A.is_equal, None, None, ["vr", "cf.27"], ["vm", "vm.t"])
-        put_nd = [(8, 1.0), (9, 2.0), (10, 4.0), (4, 8.0), (5, 16.0), (6, 32.0)]
-        prev = None
-        for i, (q, w) in enumerate(put_nd):
-            j = 50 + i % 2
-            if prev is None:
-                op("v", lambda e: e.tensor_scalar(cf(j), oh(q, q + 1), w, None, A.mult), ["oh"], c(j))
-            else:
-                op("v", lambda e: e.tensor_scalar(cf(j), oh(q, q + 1), w, cf(prev), A.mult, A.add), ["oh"] + c(prev), c(j))
-            prev = j
+        prev = c55[0]
         o = 4 * K["nd"]
-        ts(V("kt", o, o + 512, 4), V("jd", 0, 128), cf(2), A.is_equal, cf(prev), A.mult, ["jd", "cf", "kt"] + c(prev), ["kt.n0"])
-        kt_all = ["kt"] + names + ["kt.w0", "kt.w2", "kt.n0"] + ["kt.%s%d" % (x, b) for x in "op" for b in range(4)]
-        quant("kq", "ks", 0, 512, "kt", kt_all, ["kq"])
-        quant("kq", "ks", 512, 896, "kt", kt_all, ["kq.2"], 2048)
-        for a in range(4):
-            ts(V("zc", 128 * a, 128 * a + 128), V("ta", 0, 128), cf(15 + a), A.is_equal, 0.5, A.mult, ["ta", "cf.%d" % (15 + a)], ["zc.%d" % a])
-        zero("ke0", [], ["ke0"])
-        zero("ke1", [], ["ke1"])
-        for a in range(4):
-            n = "ke%d" % (a % 2)
-            for b in range(4):
-                act(V(n, 512 * b + b, 512 * b + 512, 4), V("zc", 128 * a, 128 * a + 128), ["zc.%d" % a, n], ["%s.%d" % (n, b)])
-            quant("keq", "kes", 512 * a, 512 * a + 512, n, [n] + lanes(n), ["keq.%d" % a])
-        ts(V("coff", 0, 64), V("coff", 0, 64), cf(26), A.add, None, None, ["coff", "cf.26"], ["coff"])
+        ts(V("kt", o, o + 512, 4), V("jd", 0, 128), cf(2), A.is_equal, cf(prev), A.mult, ["jd", "cf"] + z_kt + c(prev), ["kt.n0"])
+        quant("kq", "ks", 640, 896, "kt", z_kt + ["kt.w0", "kt.w2", "kt.n0"], ["kq.2"], 2560)
+        lin(V("coff", 0, 64), V("coff", 0, 64), 1.0, A.mult, cf(26), A.add, ["coff", "cf.26"], ["coff"])
         ts(V("vl", 0, 8), V("vlf", 0, 8), cf(36), A.add, None, None, ["vlf", "cf.36"], ["vl"])
-        ts(V("wl", 0, 128), V("wlf", 0, 128), cf(1), A.add, None, None, ["wlf", "cf"], ["wl"])
-        for n in ("ct", "ct2", "cc"):
-            zero(n, [], lanes(n))
-        zero("vt", [], ["vt"])
-        zero("et", [], lanes("et"))
-        quant("zq", "zs", 0, 128, "vt", ["vt"], ["zq"])
+
+    def setup_zero():
+        quant("zq", "zs", 0, 128, "z0", ["z0"], ["zq"])
         quant("vq", "vs", 0, 128, "vt0", ["vt0"], ["vq"])
         for t in range(ROUNDS):
             dma("s", lambda e: e.dma_start(V("aq%d" % t, GW, 128).bitcast(dt.uint8), V("zq", GW, 128).bitcast(dt.uint8)), ["zq"], ["aq%d" % t])
@@ -415,15 +458,15 @@ def rank_program(g, core, T, topo):
 
     fw_lanes = ["fw.%d.%d" % (b, a) for b in range(4) for a in range(4)]
 
-    def unpack():
-        i = 0
-        for a in range(4):
-            for b in range(4):
-                bank = 4 + i % 4
-                mm(bank, 256, "keq", "kes", 512 * a + 128 * b, "xq", "xs", 0, True, True, ["keq.%d" % a, "xq"])
-                o = 1024 * b + 256 * a
-                act(V("fw", o, o + 256), V("pb%d" % bank, 0, 256), ["pb%d" % bank], ["fw.%d.%d" % (b, a)])
-                i += 1
+    unpacked = [0]
+
+    def unpack_some(k):
+        for i in range(unpacked[0], unpacked[0] + k):
+            a, b, bank = i // 4, i % 4, 4 + (i + 3) % 4
+            mm(bank, 256, "keq", "kes", 512 * a + 128 * b, "xq", "xs", 0, True, True, ["keq.%d" % a, "xq"])
+            o = 1024 * b + 256 * a
+            act(V("fw", o, o + 256), V("pb%d" % bank, 0, 256), ["pb%d" % bank], ["fw.%d.%d" % (b, a)])
+        unpacked[0] = (unpacked[0] + k) % 16
 
     def d_start():
         ts(V("dh", 0, 256), V("pb2", 0, 256), cf(11), A.is_ge, cf(12), A.mult, ["pb2", "cf.11", "cf.12"], ["dh"])
@@ -434,46 +477,58 @@ def rank_program(g, core, T, topo):
 
     for t in range(ROUNDS):
         last = t == ROUNDS - 1
-        scores()
         if t == 0:
             setup_late()
-            far_scores()
-        else:
-            mm(2, 256, "kq", "ks", K["init"], "ccq", "ccs", 0, True, True, ["kq", "ccq"])
-            d_start()
-        unpack()
-        if t:
-            far_scores()
+        scores()
         tt(V("so", 0, 256), V("pb0", 0, 256), V("mask", 0, 256), A.mult, ["pb0", "mask"], ["so"])
         op("v", lambda e: e.tensor_tensor_scan(V("wsc", 0, 256), V("rst", 0, 256), V("so", 0, 256), 0.0, A.mult, A.add), ["rst", "so"], ["wsc"])
         tt(V("wm", 0, 256), ind("wsc", 0, 256, "l15", 0, 16), V("pen", 0, 256), A.add, ["wsc", "l15", "pen"], ["wm"])
-        tt(V("dtl", 0, 1024, 4), V("pb0", 0, 256), V("wm", 0, 256), A.not_equal, ["pb0", "wm"], ["dtl.0"])
-        quant("cq", "cs", 1024, 1280, "dtl", lanes("dtl"), ["cq.4"])
+        tt(V("so", 0, 256), V("pb0", 0, 256), V("wm", 0, 256), A.not_equal, ["pb0", "wm"], ["so"])
+        act(V("dtl", 0, 1024, 4), V("so", 0, 256), ["so"], ["dtl.0"], scale=2.0)
+        for el in range(4):
+            c = 12 + el
+            sc, sg = V("wsc", 16 * c + 15, 16 * c + 16), V("sg", 256 * el, 256 * el + 256)
+            op("a", lambda e: e.activation(sg, V("sw0", 0, 256), AF.Sign, bias=sc, scale=-1.0), ["sw0", "wsc"], ["sg.%d" % el])
+            op("a", lambda e: e.activation(V("cm2", el, 64 * c, 4), V("sg", 256 * el, 256 * el + 16 * c), AF.Sign, bias=cf(56), scale=-1.0), ["sg.%d" % el, "cf.56"], ["cm2.%dl" % el])
+            op("a", lambda e: e.activation(V("cm2", 64 * c + el, 1024, 4), V("sg", 256 * el + 16 * c, 256 * el + 256), AF.Sign, bias=cf(57), scale=-1.0), ["sg.%d" % el, "cf.57"], ["cm2.%dr" % el])
+        far_scores()
+        if t:
+            unpack_some(4)
         kinds = (("own", 1), ("pl", 3))
-        for m, bank in kinds:
-            mm(bank, 256, "kq", "ks", K[m], "cq", "cs", 1024, True, False, ["kq", "cq.4"])
-        for tile in range(4):
-            n = "cm%d" % (tile % 2)
-            for el in range(4):
+        for step, tile in enumerate((0, 4, 1, 2, 3)):
+            n = "cm%d" % {3: 2, 4: 9}.get(tile, tile % 2)
+            for el in range(4 if tile < 3 else 0):
                 c = 4 * tile + el
                 sc = V("wsc", 16 * c + 15, 16 * c + 16)
                 if c:
-                    ts(V(n, el, 64 * c, 4), V("pb0", 0, 16 * c), sc, A.is_gt, None, None, ["pb0", "wsc"], ["%s.%dl" % (n, el)])
-                ts(V(n, 64 * c + el, 1024, 4), V("pb0", 16 * c, 256), sc, A.is_ge, None, None, ["pb0", "wsc"], ["%s.%dr" % (n, el)])
-            quant("cq", "cs", 256 * tile, 256 * tile + 256, n, ["%s.%d%s" % (n, el, s) for el in range(4) for s in "lr"], ["cq.%d" % tile])
+                    ts(V(n, el, 64 * c, 4), V("pb0", 0, 16 * c), sc, A.is_gt, 2.0, A.mult, ["pb0", "wsc"], ["%s.%dl" % (n, el)])
+                ts(V(n, 64 * c + el, 1024, 4), V("pb0", 16 * c, 256), sc, A.is_ge, 2.0, A.mult, ["pb0", "wsc"], ["%s.%dr" % (n, el)])
+            if t == 0 and step == 0:
+                quant("kq", "ks", 0, 256, "kt", ["kt.%s%d" % (x, b) for x in "op" for b in range(4)], ["kq.1"])
+            if tile == 4:
+                quant("cq", "cs", 1024, 1280, "dtl", lanes("dtl"), ["cq.4"])
+            else:
+                quant("cq", "cs", 256 * tile, 256 * tile + 256, n, ["%s.%d%s" % (n, el, s) for el in range(4) for s in "lr"], ["cq.%d" % tile])
             for m, bank in kinds:
-                mm(bank, 256, "kq", "ks", K[m], "cq", "cs", 256 * tile, False, tile == 3, ["kq", "cq.%d" % tile])
+                mm(bank, 256, "kq", "ks", K[m], "cq", "cs", 256 * tile, step == 0, step == 4, ["kq.1", "cq.%d" % tile])
+            if t and tile == 2:
+                unpack_some(EXTRA)
+            if t == 0 and tile == 1:
+                setup_unpack(0)
+                setup_unpack(1)
+                tiles_unpack(2)
+                tiles_unpack(3)
             if t == 0 and tile == 2:
+                setup_bits()
                 for k in range(3):
                     nk = V("n%d" % k, 0, 256)
                     tt(V("ct", 1 + k, 1024, 4), nk, V("pb0", 0, 256), A.is_lt, ["pb0", "n%d" % k], lanes("ct", 1 + k))
                     tt(V("ct2", 1 + k, 1024, 4), nk, V("pb0", 0, 256), A.is_equal, ["pb0", "n%d" % k], lanes("ct2", 1 + k))
                 l = V("ct2", 1, 1024, 4)
-                tt(V("r1", 0, 256), l, V("lt0", 0, 256), A.mult, lanes("ct2", 1) + ["lt0"], ["r1"])
-                vc(l, V("r1", 0, 256), ["r1"], lanes("ct2", 1))
                 for k, j in ((1, 3), (2, 4)):
                     l2 = V("ct2", 1 + k, 1024, 4)
-                    ts(l2, l2, cf(j), A.mult, None, None, lanes("ct2", 1 + k) + ["cf"], lanes("ct2", 1 + k))
+                    act(l2, l2, lanes("ct2", 1 + k) + ["cf"], lanes("ct2", 1 + k), scale=cf(j))
+                tt(l, l, V("lt0", 0, 256), A.mult, lanes("ct2", 1) + ["lt0"], lanes("ct2", 1))
                 for i, n2 in enumerate(("ct", "ct2")):
                     quant("ctq", "cts", 256 * i, 256 * i + 256, n2, lanes(n2), ["ctq.%d" % i])
                     mm(2, 256, "kq", "ks", K["init"], "ctq", "cts", 256 * i, i == 0, i == 1, ["kq", "ctq.%d" % i])
@@ -481,10 +536,10 @@ def rank_program(g, core, T, topo):
         tt(V("bw", 0, 256), V("pb1", 0, 256), V("dh2", 0, 256), A.is_gt, ["pb1", "dh2"], ["bw"])
 
         def fill_wrap():
-            act(V("rr", 0, 256), V("pb3", 0, 256), ["pb3", "cf.33"], ["rr"], bias=cf(33))
             tt(V("r1", 0, 256), V("pb3", 0, 256), V("mask", 0, 256), A.mult, ["pb3", "mask"], ["r1"])
+            act(V("rr", 0, 256), V("pb3", 0, 256), ["pb3", "cf.33"], ["rr"], scale=0.5, bias=cf(33))
             op("v", lambda e: e.tensor_tensor_scan(V("r2", 0, 256), V("rst", 0, 256), V("r1", 0, 256), 0.0, A.mult, A.add), ["rst", "r1"], ["r2"])
-            ts(V("mu", 96, 112), V("r2", 15, 256, 16), -16.0, A.add, None, None, ["r2"], ["mu.96"])
+            ts(V("mu", 96, 112), V("r2", 15, 256, 16), 0.5, A.mult, 16.0, A.add, ["r2"], ["mu.96"])
 
         def fill_places():
             dma("s", lambda e: e.dma_start(T.tbh[:], T.rr[0:128:16, :]), ["rr"], ["tbh"])
@@ -509,8 +564,7 @@ def rank_program(g, core, T, topo):
                  T.sem["%s%d" % ("arr" if via is None else "rel", t)])
 
         def fill_turn():
-            for k in range(3):
-                op("v", lambda e: e.transpose(V("nt%d" % k, 0, 256), V("n%d" % k, 0, 256)), ["n%d" % k], ["nt%d" % k])
+            op("v", lambda e: e.transpose(V("nt", 0, 768), V("nn", 0, 768)), ["n0", "n1", "n2"], ["nt0", "nt1", "nt2"])
 
         def fill_pref():
             nt = [V("nt%d" % k, 0, 256, 16) for k in range(3)]
@@ -520,10 +574,10 @@ def rank_program(g, core, T, topo):
             tt(P(0), P(3), P(4), A.add, ["pw.3", "pw.4"], ["pw.0"])
             tt(P(1), P(5), P(3), A.subtract, ["pw.5", "pw.3"], ["pw.1"])
             tt(P(2), P(4), P(5), A.add, ["pw.4", "pw.5"], ["pw.2"])
-            ts(P(0), P(0), 1.0, A.add, None, None, ["pw.0"], ["pw.0"])
-            ts(P(1), P(1), 2.0, A.add, None, None, ["pw.1"], ["pw.1"])
-            ts(P(2), P(2), -1.0, A.mult, 3.0, A.add, ["pw.2"], ["pw.2"])
-        fills = [fill_wrap, fill_places, fill_gate, fill_send, fill_turn, fill_pref]
+            for k, w, j in ((0, 1.0, 58), (1, 1.0, 59), (2, -1.0, 60)):
+                act(P(k), P(k), ["pw.%d" % k, "cf.%d" % j], ["pw.%d" % k], scale=w, bias=cf(j))
+        fills = [fill_wrap, fill_places, fill_turn, fill_pref, fill_gate, fill_send]
+        some = (4, 4, 4, 4) if t == 0 else SOME
 
         for i in range(SWEEPS):
             vc(V("st", 0, 1024, 4), V("bw", 0, 256), ["bw"], lanes("st", 0))
@@ -533,11 +587,20 @@ def rank_program(g, core, T, topo):
             quant("sq", "ss", 0, 256, "st", lanes("st"), ["sq"])
             m = "fin" if i == SWEEPS - 1 else "s"
             mm(2, 256, "kq", "ks", K[m], "sq", "ss", 0, True, True, ["kq", "kq.2", "sq"])
-            if i < len(fills):
-                fills[i]()
-            if t == 0 and i == 3:
-                layers()
-                zero("hw", [], hw_lanes)
+            if t == 0 and i == 0:
+                setup_unpack(2)
+                setup_unpack(3)
+            fills[i]()
+            if i < 4:
+                unpack_some(some[i])
+            if t == 0:
+                if i == 1:
+                    setup_zero()
+                if i == 4:
+                    ts(V("wl", 0, 128), V("wlf", 0, 128), cf(1), A.add, None, None, ["wlf", "cf"], ["wl"])
+                    layers()
+                if i == 5:
+                    setup_routes()
             ts(V("bw", 0, 256), V("pb2", 0, 256), cf(11) if m == "s" else -0.5, A.is_lt, None, None, ["pb2", "cf.11"], ["bw"])
         op("v", lambda e: e.transpose(V("bt", 0, 256), V("bw", 0, 256)), ["bw"], ["bt"])
         tk = lambda i: V("tk", 16 * i, 16 * i + 16)
@@ -550,6 +613,10 @@ def rank_program(g, core, T, topo):
         tt(V("vt", 0, 256, 2), ind("eqk", 0, 32, "vl", 0, 8), V("vm", 0, 128), A.mult, ["eqk.0", "eqk.1", "vl", "vm"], ["vt"])
         quant("vtq", "vts", 0, 128, "vt", ["vt"], ["vtq"])
         mm(0, 128, "kq", "ks", K["kw"], "vtq", "vts", 0, True, True, ["kq.2", "vtq"])
+        act(V("cc", 0, 1024, 4), V("bw", 0, 256), ["bw"], lanes("cc", 0))
+        quant("ccq", "ccs", 0, 256, "cc", lanes("cc"), ["ccq"])
+        if not last:
+            mm(2, 256, "kq", "ks", K["init"], "ccq", "ccs", 0, True, True, ["kq", "ccq"])
         tt(V("of", 0, 64), V("pb0", 0, 64), V("coff", 0, 64), A.add, ["pb0", "coff"], ["of"])
         vc(V("ou", 0, 64), V("of", 0, 64), ["of"], ["ou"])
         l4 = ["l4.0", "l4.1"]
@@ -568,6 +635,8 @@ def rank_program(g, core, T, topo):
                 o = 1024 * b + 256 * a
                 act(V("hw", o, o + GW), V("pb%d" % bank, 0, GW), ["pb%d" % bank], ["hw.%d.%d" % (b, a)], scale=0.015625)
                 i += 1
+        if not last:
+            d_start()
         pick("da", "mu", 0, 16, "mu", 16, "mu.0")
         pick("da", "mu", 16, 32, "mu", 32, "mu.16")
         pick("da", "mu", 32, 48, "mu", 48, "mu.32")
@@ -579,8 +648,6 @@ def rank_program(g, core, T, topo):
             tt(V("xn", b, 1024, 4), ind("hw", 1024 * b, 1024 * b + 1024, "mu", 64, 80), V("zb", 256 * b, 256 * b + 256), A.add,
                hw_lanes + ["mu.64", "zb.%d" % b], lanes("xn", b))
         quant("xq", "xs", 0, 256, "xn", lanes("xn"), ["xq"])
-        vc(V("cc", 0, 1024, 4), V("bw", 0, 256), ["bw"], lanes("cc", 0))
-        quant("ccq", "ccs", 0, 256, "cc", lanes("cc"), ["ccq"])
         if last:
             dma("s", lambda e: e.dma_start(T.oc[:, :], T.xq[:].bitcast(dt.uint8)), ["xq"], ["out.oc"])
             for k in range(4):

@@ -22,7 +22,7 @@ SCRATCH = {
     "keq": ("sbuf", [128, 2048], F8), "kes": ("sbuf", [128, 2048], U8), "lt0": ("sbuf", [128, 256], F32),
     "sw": ("sbuf", [128, 768], F32), "nn": ("sbuf", [128, 768], F32), "nt": ("sbuf", [128, 768], F32), "pw": ("sbuf", [128, 96], F32),
     "so": ("sbuf", [128, 256], F32), "wsc": ("sbuf", [128, 256], F32), "wm": ("sbuf", [128, 256], F32), "dtl": ("sbuf", [128, 1024], BF),
-    "cm0": ("sbuf", [128, 1024], BF), "cm2": ("sbuf", [128, 1024], BF), "sg": ("sbuf", [128, 1024], BF), "cm1": ("sbuf", [128, 1024], BF), "cq": ("sbuf", [128, 1280], F8), "cs": ("sbuf", [128, 1280], U8),
+    "cm0": ("sbuf", [128, 1024], BF), "cm3": ("sbuf", [128, 1024], BF), "cm2": ("sbuf", [128, 1024], BF), "sg": ("sbuf", [128, 1024], BF), "cm1": ("sbuf", [128, 1024], BF), "cq": ("sbuf", [128, 1280], F8), "cs": ("sbuf", [128, 1280], U8),
     "ct": ("sbuf", [128, 1024], BF), "ct2": ("sbuf", [128, 1024], BF), "cc": ("sbuf", [128, 1024], BF), "ctq": ("sbuf", [128, 512], F8), "cts": ("sbuf", [128, 512], U8),
     "ccq": ("sbuf", [128, 256], F8), "ccs": ("sbuf", [128, 256], U8), "dh": ("sbuf", [128, 256], F32), "dh2": ("sbuf", [128, 256], F32),
     "bw": ("sbuf", [128, 256], BF), "st": ("sbuf", [128, 1024], BF), "sq": ("sbuf", [128, 256], F8), "ss": ("sbuf", [128, 256], U8),
@@ -43,7 +43,8 @@ for _n, _w, _k in (("pb", 512, 8), ("sw", 256, 3), ("n", 256, 3), ("nt", 256, 3)
     for _i in range(_k):
         PIECE["%s%d" % (_n, _i)] = ("nn" if _n == "n" else _n, _w * _i)
 SEMAPHORES = ["qv", "qa", "qt", "qp", "loc"] + ["arr%d" % i for i in range(ROUNDS)] + ["rel%d" % i for i in range(ROUNDS)] + ["d%d" % i for i in range(64)]
-EXTRA, SOME = 1, (2, 3, 3, 3)
+ON_SCALAR = (10, 11, 12, 13, 14, 15)
+OFF = 32 - 16 * len(ON_SCALAR)
 NE = 4
 
 
@@ -296,9 +297,6 @@ def rank_program(g, core, T, topo):
     op("v", lambda e: e.tensor_copy(V("up", 0, 384).bitcast(dt.uint32), V("uq", 0, 128).bitcast(dt.uint32).indirect(V("ul", 0, 24))), ["uq", "ul"], ["up"])
     op("a", lambda e: e.activation(V("ups", 0, 384), ind("us", 0, 128, "ul", 0, 24), AF.Copy), ["uq", "ul"], ["ups"])
     quant("xq", "xs", 0, 256, "xt", ["xt"], ["xq"])
-    for b in range(4):
-        act(V("kt", b, 512, 4), V("kc", 0, 128), ["kc"], ["kt.o%d" % b])
-        act(V("kt", 512 + b, 1024, 4), V("kp", 0, 128), ["kp"], ["kt.p%d" % b])
     c55 = []
 
     def setup_unpack(a):
@@ -327,8 +325,6 @@ def rank_program(g, core, T, topo):
 
     def setup_late():
         oh = lambda a, b: V("oh", a, b)
-        for b in range(4):
-            act(V("bx4", b, 512, 4), V("blkx", 0, 128), ["blkx"], lanes("bx4", b))
         cs_(49, 7, 16.0, A.mult, cf(9), A.add)
         ts(V("ql", 0, 32), V("qlf", 0, 32), cf(49), A.add, None, None, ["qlf", "cf.49"], ["ql"])
         cs_(28, 3, 256.0, A.mult)
@@ -337,7 +333,7 @@ def rank_program(g, core, T, topo):
         cs_(6, 4, 512.0, A.mult, cf(28), A.add, ["cf.28"])
         cs_(24, 4, 512.0, A.mult, cf(29), A.add, ["cf.29"])
         cs_(8 + 24, 4, -512.0, A.mult, cf(30), A.add, ["cf.30"])
-        cs_(33, 6, 16.0, A.add, rd=["cf.6"])
+        cs_(33, 6, -0.5 * OFF, A.add, rd=["cf.6"])
         cs_(34, 5, 512.0, A.mult)
         cs_(26, 1, 64.0, A.mult)
         cs_(27, 6, 1.0 / 256.0, A.mult, rd=["cf.6"])
@@ -362,9 +358,10 @@ def rank_program(g, core, T, topo):
         cs_(37, 22, -0.5, A.add, rd=c(22))
         lin(cf(11), oh(7, 8), -2.0, A.mult, cf(37), A.add, ["oh"] + c(37), c(11))
         lin(cf(12), oh(11, 12), -1e4, A.mult, 1e4, A.add, ["oh"], c(12))
-        cs_(38, 22, oh(7, 8), A.add, 295.0, A.mult, c(22) + ["oh"])
+        edge = 127.0 + OFF
+        cs_(38, 22, oh(7, 8), A.add, edge + 200.0, A.mult, c(22) + ["oh"])
         cs_(39, 38, -200.0, A.add, rd=c(38))
-        lin(cf(13), oh(11, 12), 105.0, A.mult, cf(39), A.add, ["oh"] + c(39), c(13))
+        lin(cf(13), oh(11, 12), 200.0 - edge, A.mult, cf(39), A.add, ["oh"] + c(39), c(13))
         tt(V("mm3", 0, 3), oh(0, 3), oh(8, 11), A.add, ["oh"], ["mm3.0"])
         tt(V("mm3", 4, 7), oh(4, 7), oh(8, 11), A.add, ["oh"], ["mm3.1"])
         tt(cf(40), oh(3, 4), oh(7, 8), A.add, ["oh"], c(40))
@@ -416,6 +413,11 @@ def rank_program(g, core, T, topo):
             lin(cf(j), oh(q, q + 1), w, A.mult, cf(prev) if prev else None, A.add if prev else None, ["oh"] + (c(prev) if prev else []), c(j))
             prev = j
         c55.append(prev)
+        for b in range(4):
+            act(V("kt", b, 512, 4), V("kc", 0, 128), ["kc"], ["kt.o%d" % b])
+            act(V("kt", 512 + b, 1024, 4), V("kp", 0, 128), ["kp"], ["kt.p%d" % b])
+        for b in range(4):
+            act(V("bx4", b, 512, 4), V("blkx", 0, 128), ["blkx"], lanes("bx4", b))
 
     def setup_bits():
         for i, m in enumerate(("s", "fin", "init")):
@@ -460,10 +462,14 @@ def rank_program(g, core, T, topo):
 
     unpacked = [0]
 
-    def unpack_some(k):
+    def unpack_products(k):
         for i in range(unpacked[0], unpacked[0] + k):
             a, b, bank = i // 4, i % 4, 4 + (i + 3) % 4
             mm(bank, 256, "keq", "kes", 512 * a + 128 * b, "xq", "xs", 0, True, True, ["keq.%d" % a, "xq"])
+
+    def unpack_casts(k):
+        for i in range(unpacked[0], unpacked[0] + k):
+            a, b, bank = i // 4, i % 4, 4 + (i + 3) % 4
             o = 1024 * b + 256 * a
             act(V("fw", o, o + 256), V("pb%d" % bank, 0, 256), ["pb%d" % bank], ["fw.%d.%d" % (b, a)])
         unpacked[0] = (unpacked[0] + k) % 16
@@ -485,20 +491,23 @@ def rank_program(g, core, T, topo):
         tt(V("wm", 0, 256), ind("wsc", 0, 256, "l15", 0, 16), V("pen", 0, 256), A.add, ["wsc", "l15", "pen"], ["wm"])
         tt(V("so", 0, 256), V("pb0", 0, 256), V("wm", 0, 256), A.not_equal, ["pb0", "wm"], ["so"])
         act(V("dtl", 0, 1024, 4), V("so", 0, 256), ["so"], ["dtl.0"], scale=2.0)
-        for el in range(4):
-            c = 12 + el
-            sc, sg = V("wsc", 16 * c + 15, 16 * c + 16), V("sg", 256 * el, 256 * el + 256)
+        for c in ON_SCALAR:
+            el, n, s = c % 4, "cm%d" % {2: 3, 3: 2}[c // 4], 256 * (c % 4)
+            sc, sg = V("wsc", 16 * c + 15, 16 * c + 16), V("sg", s, s + 256)
             op("a", lambda e: e.activation(sg, V("sw0", 0, 256), AF.Sign, bias=sc, scale=-1.0), ["sw0", "wsc"], ["sg.%d" % el])
-            op("a", lambda e: e.activation(V("cm2", el, 64 * c, 4), V("sg", 256 * el, 256 * el + 16 * c), AF.Sign, bias=cf(56), scale=-1.0), ["sg.%d" % el, "cf.56"], ["cm2.%dl" % el])
-            op("a", lambda e: e.activation(V("cm2", 64 * c + el, 1024, 4), V("sg", 256 * el + 16 * c, 256 * el + 256), AF.Sign, bias=cf(57), scale=-1.0), ["sg.%d" % el, "cf.57"], ["cm2.%dr" % el])
+            op("a", lambda e: e.activation(V(n, el, 64 * c, 4), V("sg", s, s + 16 * c), AF.Sign, bias=cf(56), scale=-1.0), ["sg.%d" % el, "cf.56"], ["%s.%dl" % (n, el)])
+            op("a", lambda e: e.activation(V(n, 64 * c + el, 1024, 4), V("sg", s + 16 * c, s + 256), AF.Sign, bias=cf(57), scale=-1.0), ["sg.%d" % el, "cf.57"], ["%s.%dr" % (n, el)])
         far_scores()
         if t:
-            unpack_some(4)
+            unpack_products(4)
+            unpack_casts(4)
         kinds = (("own", 1), ("pl", 3))
         for step, tile in enumerate((0, 4, 1, 2, 3)):
-            n = "cm%d" % {3: 2, 4: 9}.get(tile, tile % 2)
-            for el in range(4 if tile < 3 else 0):
+            n = "cm%d" % (tile if tile < 2 else {2: 3, 3: 2, 4: 9}[tile])
+            for el in range(4 if tile < 4 else 0):
                 c = 4 * tile + el
+                if c in ON_SCALAR:
+                    continue
                 sc = V("wsc", 16 * c + 15, 16 * c + 16)
                 if c:
                     ts(V(n, el, 64 * c, 4), V("pb0", 0, 16 * c), sc, A.is_gt, 2.0, A.mult, ["pb0", "wsc"], ["%s.%dl" % (n, el)])
@@ -511,8 +520,6 @@ def rank_program(g, core, T, topo):
                 quant("cq", "cs", 256 * tile, 256 * tile + 256, n, ["%s.%d%s" % (n, el, s) for el in range(4) for s in "lr"], ["cq.%d" % tile])
             for m, bank in kinds:
                 mm(bank, 256, "kq", "ks", K[m], "cq", "cs", 256 * tile, step == 0, step == 4, ["kq.1", "cq.%d" % tile])
-            if t and tile == 2:
-                unpack_some(EXTRA)
             if t == 0 and tile == 1:
                 setup_unpack(0)
                 setup_unpack(1)
@@ -535,11 +542,13 @@ def rank_program(g, core, T, topo):
                 d_start()
         tt(V("bw", 0, 256), V("pb1", 0, 256), V("dh2", 0, 256), A.is_gt, ["pb1", "dh2"], ["bw"])
 
-        def fill_wrap():
+        def fill_mask():
             tt(V("r1", 0, 256), V("pb3", 0, 256), V("mask", 0, 256), A.mult, ["pb3", "mask"], ["r1"])
             act(V("rr", 0, 256), V("pb3", 0, 256), ["pb3", "cf.33"], ["rr"], scale=0.5, bias=cf(33))
+
+        def fill_wrap():
             op("v", lambda e: e.tensor_tensor_scan(V("r2", 0, 256), V("rst", 0, 256), V("r1", 0, 256), 0.0, A.mult, A.add), ["rst", "r1"], ["r2"])
-            ts(V("mu", 96, 112), V("r2", 15, 256, 16), 0.5, A.mult, 16.0, A.add, ["r2"], ["mu.96"])
+            ts(V("mu", 96, 112), V("r2", 15, 256, 16), 0.5, A.mult, -0.5 * OFF, A.add, ["r2"], ["mu.96"])
 
         def fill_places():
             dma("s", lambda e: e.dma_start(T.tbh[:], T.rr[0:128:16, :]), ["rr"], ["tbh"])
@@ -548,10 +557,12 @@ def rank_program(g, core, T, topo):
                     ["tbh", "ci.%d" % (10 + h)], ["ho.%d" % h])
             op("v", lambda e: e.tensor_copy(V("lw", 0, 256).indirect(V("mu", 96, 112)), V("jrow", 0, 256)), ["mu.96", "jrow"], ["lw"])
 
-        def fill_gate():
+        def fill_list():
             tt(V("r1", 0, 64), V("lw", 0, 64), V("mask", 0, 64), A.mult, ["lw", "mask"], ["r1"])
             op("v", lambda e: e.tensor_tensor_scan(V("r2", 0, 64), V("rst", 0, 64), V("r1", 0, 64), 0.0, A.mult, A.add), ["rst", "r1"], ["r2"])
             ts(V("mu", 112, 116), V("r2", 15, 64, 16), cf(6), A.add, None, None, ["r2", "cf.6"], ["mu.112"])
+
+        def fill_gate():
             for b in range(4):
                 act(V("et", b, 256, 4), ind("fw", 1024 * b, 1024 * b + 1024, "mu", 112, 116), fw_lanes + ["mu.112"], lanes("et", b), scale=2.0)
 
@@ -563,36 +574,44 @@ def rank_program(g, core, T, topo):
             send(g, T, topo, core, to, V("%sq%d" % (p, t), 0, GW), V("eq%d" % t, 0, GW), V("%ss%d" % (p, t), 0, GW), V("es%d" % t, 0, GW),
                  T.sem["%s%d" % ("arr" if via is None else "rel", t)])
 
-        def fill_turn():
-            op("v", lambda e: e.transpose(V("nt", 0, 768), V("nn", 0, 768)), ["n0", "n1", "n2"], ["nt0", "nt1", "nt2"])
+        def fill_turn(k):
+            op("v", lambda e: e.transpose(V("nt%d" % k, 0, 256), V("n%d" % k, 0, 256)), ["n%d" % k], ["nt%d" % k])
 
         def fill_pref():
             nt = [V("nt%d" % k, 0, 256, 16) for k in range(3)]
             P = lambda i: V("pw", 16 * i, 16 * i + 16)
             for i, (x, y) in enumerate(((0, 1), (0, 2), (1, 2))):
                 tt(P(3 + i), nt[x], nt[y], A.is_le, ["nt%d" % x, "nt%d" % y], ["pw.%d" % (3 + i)])
+
+        def fill_weigh():
+            P = lambda i: V("pw", 16 * i, 16 * i + 16)
             tt(P(0), P(3), P(4), A.add, ["pw.3", "pw.4"], ["pw.0"])
             tt(P(1), P(5), P(3), A.subtract, ["pw.5", "pw.3"], ["pw.1"])
             tt(P(2), P(4), P(5), A.add, ["pw.4", "pw.5"], ["pw.2"])
             for k, w, j in ((0, 1.0, 58), (1, 1.0, 59), (2, -1.0, 60)):
                 act(P(k), P(k), ["pw.%d" % k, "cf.%d" % j], ["pw.%d" % k], scale=w, bias=cf(j))
-        fills = [fill_wrap, fill_places, fill_turn, fill_pref, fill_gate, fill_send]
-        some = (4, 4, 4, 4) if t == 0 else SOME
+        before = [[fill_mask], [lambda: fill_turn(0)], [lambda: fill_turn(1)], [lambda: fill_turn(2)], [], [fill_send]]
+        after = [[fill_wrap], [fill_places], [fill_list], [fill_pref], [fill_gate, fill_weigh], []]
+        some = (4, 4, 4, 4) if t == 0 else (3, 3, 3, 3)
 
         for i in range(SWEEPS):
+            if i < 4:
+                unpack_products(some[i])
             vc(V("st", 0, 1024, 4), V("bw", 0, 256), ["bw"], lanes("st", 0))
             for k in (1, 2):
                 act(V("st", 1 + k, 1024, 4), ind("bw", 0, 256, "lku", 16 * k, 16 * k + 16), ["bw", "lku"], lanes("st", 1 + k))
             vc(V("st", 1, 1024, 4), ind("bw", 0, 256, "lku", 0, 16), ["bw", "lku"], lanes("st", 1))
+            if i < 4:
+                unpack_casts(some[i])
+            for f in before[i]:
+                f()
             quant("sq", "ss", 0, 256, "st", lanes("st"), ["sq"])
             m = "fin" if i == SWEEPS - 1 else "s"
             mm(2, 256, "kq", "ks", K[m], "sq", "ss", 0, True, True, ["kq", "kq.2", "sq"])
-            if t == 0 and i == 0:
-                setup_unpack(2)
-                setup_unpack(3)
-            fills[i]()
-            if i < 4:
-                unpack_some(some[i])
+            if t == 0 and i < 2:
+                setup_unpack(2 + i)
+            for f in after[i]:
+                f()
             if t == 0:
                 if i == 1:
                     setup_zero()

from concourse.bass import IndirectOffsetOnAxis
from concourse.mybir import dt, AluOpType, AxisListType, ActivationFunctionType

N, C, GW, ROUNDS, SWEEPS = 8, 256, 64, 3, 6
F8, F32, BF, I32, U16, U8 = "float8_e4m3fn_x4", "float32", "bfloat16", "int32", "uint16", "uint8"
SCRATCH = {
    "xt": ("sbuf", [128, 1024], BF), "xn": ("sbuf", [128, 1024], BF), "ut": ("sbuf", [128, 512], BF), "vt0": ("sbuf", [128, 512], BF),
    "lki": ("sbuf", [128, 48], I32), "lku": ("sbuf", [128, 48], U16), "lkf": ("sbuf", [128, 48], F32), "lkx": ("sbuf", [128, 64], F32),
    "tbl": ("dram", [4, 2048], F32), "l4": ("sbuf", [128, 4096], F32), "tbh": ("dram", [4, 512], F32), "ho": ("sbuf", [128, 1024], F32),
    "xq": ("sbuf", [128, 256], F8), "xs": ("sbuf", [128, 256], U8), "uq": ("sbuf", [128, 128], F8), "us": ("sbuf", [128, 128], U8),
    "up": ("sbuf", [128, 384], F8), "ups": ("sbuf", [128, 384], U8), "vq": ("sbuf", [128, 128], F8), "vs": ("sbuf", [128, 128], U8),
    "wq": ("sbuf", [128, 512], F8), "wsx": ("sbuf", [128, 512], U8), "wp": ("sbuf", [128, 2048], F8), "wps": ("sbuf", [128, 2048], U8),
    "ci": ("sbuf", [128, 16], I32), "cf": ("sbuf", [128, 64], F32), "jm": ("sbuf", [128, 256], F32), "jd": ("sbuf", [128, 128], F32),
    "jrow": ("sbuf", [128, 256], F32), "gx": ("sbuf", [128, 128], F32), "gc": ("sbuf", [128, 128], F32), "half": ("sbuf", [128, 64], BF), "z0": ("sbuf", [128, 1024], BF), "qlf": ("sbuf", [128, 32], F32), "bx4": ("sbuf", [128, 512], F32),
    "ulf": ("sbuf", [128, 24], F32), "ul": ("sbuf", [128, 24], U16), "wlf": ("sbuf", [128, 128], F32), "wl": ("sbuf", [128, 128], U16),
    "t16": ("sbuf", [128, 16], F32), "l15": ("sbuf", [128, 16], U16), "m0": ("sbuf", [128, 16], U16), "ql": ("sbuf", [128, 32], U16),
    "coff": ("sbuf", [128, 64], F32), "vlf": ("sbuf", [128, 8], F32), "vl": ("sbuf", [128, 8], U16), "vr": ("sbuf", [128, 128], F32),
    "vm": ("sbuf", [128, 128], F32), "mask": ("sbuf", [128, 256], F32), "rst": ("sbuf", [128, 256], F32), "pen": ("sbuf", [128, 256], F32),
    "oh": ("sbuf", [128, 16], F32), "rb": ("sbuf", [128, 192], F32), "mm3": ("sbuf", [128, 8], F32), "blkx": ("sbuf", [128, 128], F32),
    "kc": ("sbuf", [128, 128], BF), "kp": ("sbuf", [128, 128], BF), "kt": ("sbuf", [128, 3584], BF), "kq": ("sbuf", [128, 896], F8), "ks": ("sbuf", [128, 896], U8),
    "ke0": ("sbuf", [128, 2048], BF), "ke1": ("sbuf", [128, 2048], BF),
    "keq": ("sbuf", [128, 2048], F8), "kes": ("sbuf", [128, 2048], U8), "lt0": ("sbuf", [128, 256], F32),
    "sw": ("sbuf", [128, 768], F32), "nn": ("sbuf", [128, 768], F32), "nt": ("sbuf", [128, 768], F32), "pw": ("sbuf", [128, 96], F32),
    "so": ("sbuf", [128, 256], F32), "wsc": ("sbuf", [128, 256], F32), "wm": ("sbuf", [128, 256], F32), "dtl": ("sbuf", [128, 1024], BF),
    "cm0": ("sbuf", [128, 1024], BF), "cm3": ("sbuf", [128, 1024], BF), "cm2": ("sbuf", [128, 1024], BF), "sg": ("sbuf", [128, 1024], BF), "cm1": ("sbuf", [128, 1024], BF), "cq": ("sbuf", [128, 1280], F8), "cs": ("sbuf", [128, 1280], U8),
    "ct": ("sbuf", [128, 1024], BF), "ct2": ("sbuf", [128, 1024], BF), "cc": ("sbuf", [128, 1024], BF), "ctq": ("sbuf", [128, 512], F8), "cts": ("sbuf", [128, 512], U8),
    "ccq": ("sbuf", [128, 256], F8), "ccs": ("sbuf", [128, 256], U8), "dh": ("sbuf", [128, 256], F32), "dh2": ("sbuf", [128, 256], F32),
    "bw": ("sbuf", [128, 256], BF), "st": ("sbuf", [128, 1024], BF), "sq": ("sbuf", [128, 256], F8), "ss": ("sbuf", [128, 256], U8),
    "bt": ("sbuf", [128, 256], BF), "tk": ("sbuf", [128, 80], F32), "eqk": ("sbuf", [128, 32], F32), "vt": ("sbuf", [128, 512], BF),
    "vtq": ("sbuf", [128, 128], F8), "vts": ("sbuf", [128, 128], U8), "of": ("sbuf", [128, 64], F32), "ou": ("sbuf", [128, 64], U16),
    "da": ("sbuf", [128, 1024], F32), "hp": ("sbuf", [128, 256], F32), "hs": ("sbuf", [128, 256], F32), "mu": ("sbuf", [128, 128], U16),
    "rr": ("sbuf", [128, 256], F32), "r1": ("sbuf", [128, 256], F32), "r2": ("sbuf", [128, 256], F32), "lw": ("sbuf", [128, 256], F32),
    "fw": ("sbuf", [128, 4096], BF), "hw": ("sbuf", [128, 4096], BF), "fd": ("sbuf", [128, 1024], BF), "zb": ("sbuf", [128, 1024], BF),
    "et": ("sbuf", [128, 512], BF), "zq": ("sbuf", [128, 128], F8), "zs": ("sbuf", [128, 128], U8),
    "ys": ("sbuf", [128, 256], F32), "ndb": ("sbuf", [128, 512], F32), "ev": ("sbuf", [128, 512], F32),
}
SCRATCH["pb"] = ("psum", [128, 4096], F32)
for _n, _w in (("e", 128), ("r", GW), ("a", 128)):
    SCRATCH[_n + "q"] = ("sbuf", [128, _w * ROUNDS], F8)
    SCRATCH[_n + "s"] = ("sbuf", [128, _w * ROUNDS], U8)
PIECE = {}
for _n, _w, _k in (("pb", 512, 8), ("sw", 256, 3), ("n", 256, 3), ("nt", 256, 3), ("eq", 128, 3), ("es", 128, 3), ("rq", GW, 3), ("rs", GW, 3), ("aq", 128, 3), ("as", 128, 3)):
    for _i in range(_k):
        PIECE["%s%d" % (_n, _i)] = ("nn" if _n == "n" else _n, _w * _i)
SEMAPHORES = ["qv", "qa", "qt", "qp", "loc"] + ["arr%d" % i for i in range(ROUNDS)] + ["rel%d" % i for i in range(ROUNDS)] + ["d%d" % i for i in range(64)]
ON_SCALAR = (10, 11, 12, 13, 14, 15)
OFF = 32 - 16 * len(ON_SCALAR)
NE = 4


def view(T, n, a, b, st=1):
    n, o = PIECE.get(n, (n, 0))
    return T[n][:, o + a:o + b] if st == 1 else T[n][:, o + a:o + b:st]


def mask_of(topo, src, dst):
    return sum(1 << e for e in topo.engines(src, dst)[:NE])


def helper_of(topo, src, dst):
    if topo.may_write(src, dst):
        return None
    able = [c for c in topo.cores_of(src) if c != src and topo.may_write(c, dst)]
    near = [c for c in able if topo.die(c) == topo.die(src)]
    return (near or able)[0]


def send(g, T, topo, src, dst, q_out, q_in, s_out, s_in, sem):
    rid, pid = topo.addr(dst, src)
    m = mask_of(topo, src, dst)
    g.remote_dma(q_out.bitcast(dt.uint8), q_in.bitcast(dt.uint8), sem, T.sem.loc, pid, rid, m)
    g.remote_dma(s_out, s_in, sem, T.sem.loc, pid, rid, m)


def rank_program(g, core, T, topo):
    rank = T.rank_of(core)
    if rank is None:
        n = 0
        for i in range(N):
            src, dst = T.cores[i], T.cores[(i + 1) % N]
            if helper_of(topo, src, dst) != core:
                continue
            for t in range(ROUNDS):
                g.wait_ge(T.sem["rel%d" % t], 2 * NE)
                send(g, T, topo, core, dst, view(T, "aq%d" % t, 0, GW), view(T, "rq%d" % t, 0, GW), view(T, "as%d" % t, 0, GW), view(T, "rs%d" % t, 0, GW), T.sem["arr%d" % t])
                n += 2 * NE
        if n:
            g.wait_ge(T.sem.loc, n)
        return

    A, AF = AluOpType, ActivationFunctionType
    Q = {"v": g.vector, "a": g.scalar, "t": g.tensor, "g": g, "s": g.sync}
    SRC = {"v": "qv", "a": "qa", "t": "qt", "g": "qp"}
    cnt = {}
    known = {q: {} for q in Q}
    clk = {}
    wrote, read = {}, {}
    ndma = [0]

    def waits(q, rd, wr, free=False):
        need = {}

        def want(e):
            if e[0] == SRC.get(q) and (free or q == "t"):
                return
            if need.get(e[0], 0) < e[1]:
                need[e[0]] = e[1]
        for r in rd:
            if r in wrote:
                e = wrote[r]
                if not (e[0] == SRC.get(q) and q == "t"):
                    if need.get(e[0], 0) < e[1]:
                        need[e[0]] = e[1]
            if r[:2] == "pb":
                for s, k in read.get(r, {}).items():
                    if s != SRC.get(q):
                        want((s, k))
        for w in wr:
            if w in wrote:
                want(wrote[w])
            for s, k in read.get(w, {}).items():
                want((s, k))
        need = {s: k for s, k in need.items() if known[q].get(s, 0) < k}
        for s, k in sorted(need.items()):
            if any(s2 != s and clk[(s2, k2)].get(s, 0) >= k for s2, k2 in need.items()):
                continue
            Q[q].wait_ge(T.sem[s], k)
        for s, k in need.items():
            for s2, k2 in clk[(s, k)].items():
                if known[q].get(s2, 0) < k2:
                    known[q][s2] = k2
            if known[q].get(s, 0) < k:
                known[q][s] = k

    def done(e, rd, wr, q):
        clk[e] = dict(known[q])
        for r in rd:
            read.setdefault(r, {})[e[0]] = e[1]
        for w in wr:
            wrote[w] = e
            read[w] = {}

    def op(q, fn, rd, wr, free=False):
        waits(q, rd, wr, free)
        s = SRC[q]
        cnt[s] = cnt.get(s, 0) + 1
        fn(Q[q]).then_inc(T.sem[s], 1)
        done((s, cnt[s]), rd, wr, q)

    def dma(q, fn, rd, wr):
        waits(q, rd, wr)
        s = "d%d" % ndma[0]
        ndma[0] += 1
        cnt[s] = 16
        fn(Q[q]).then_inc(T.sem[s], 16)
        done((s, 16), rd, wr, q)

    def V(n, a, b, st=1):
        return view(T, n, a, b, st)

    def lanes(n, *ls):
        return [n + "." + str(x) for x in (ls or (0, 1, 2, 3))]

    def ts(out, in0, s1, o0, s2=None, o1=None, rd=(), wr=(), free=False):
        if s2 is None:
            op("v", lambda e: e.tensor_scalar(out, in0, s1, None, o0), list(rd), list(wr), free)
        else:
            op("v", lambda e: e.tensor_scalar(out, in0, s1, s2, o0, o1), list(rd), list(wr), free)

    def tt(out, a, b, o, rd=(), wr=(), free=False):
        op("v", lambda e: e.tensor_tensor(out, a, b, o), list(rd), list(wr), free)

    def vc(out, in_, rd=(), wr=(), free=False):
        op("v", lambda e: e.tensor_copy(out, in_), list(rd), list(wr), free)

    def act(out, in_, rd=(), wr=(), scale=1.0, bias=None):
        if bias is None:
            op("a", lambda e: e.activation(out, in_, AF.Copy, scale=scale), list(rd), list(wr))
        else:
            op("a", lambda e: e.activation(out, in_, AF.Identity, bias=bias, scale=scale), list(rd), list(wr))

    def iota(n, a, b, pat, base=0, cm=0, st=1):
        f = SCRATCH[n][2] == F32
        if f:
            op("g", lambda e: e.iota(V(n, a, b, st), pat, base, cm, allow_small_or_imprecise_dtypes=True), [], [n], True)
        else:
            op("g", lambda e: e.iota(V(n, a, b, st), pat, base, cm), [], [n], True)

    def zero(n, rd, wr):
        op("v", lambda e: e.memset(T[n][:], 0.0), rd, wr)

    def quant(cq, cs, a, b, tile, rd, wr, ta=0):
        op("v", lambda e: e.quantize_mx(V(cq, a, b), V(cs, a, b), V(tile, ta, ta + 4 * (b - a))), rd, wr)

    def mm(bank, n, lq, ls, la, rq, rs, ra, start, stop, rd):
        op("t", lambda e: e.matmul_mx(V("pb%d" % bank, 0, n), V(lq, la, la + 128), V(ls, la, la + 128), V(rq, ra, ra + n), V(rs, ra, ra + n), start, stop),
           rd, ["pb%d" % bank])

    def clear(n, w, wr):
        for a in range(0, w, 1024):
            k = min(1024, w - a)
            dma("s", lambda e: e.dma_start(V(n, a, a + k), V("z0", 0, k)), ["z0"], [wr + "/%d" % a])
        return [wr + "/%d" % a for a in range(0, w, 1024)]

    def ind(n, a, b, off, oa, ob):
        return V(n, a, b).indirect(V(off, oa, ob))

    K = {"own": 0, "pl": 128, "init": 256, "s": 384, "fin": 512, "kw": 640, "nd": 768}

    dma("s", lambda e: e.dma_start(T.ut[:], T.u[:, :]), [], ["ut"])
    dma("a", lambda e: e.dma_start(T.xt[:], T.x[:, :]), [], ["xt"])
    dma("s", lambda e: e.dma_start(T.lki[:], T.lk[:, :]), [], ["lki"])
    dma("a", lambda e: e.dma_start(T.wq[:].bitcast(dt.uint8), T.wc[:, :]), [], ["wq"])
    dma("s", lambda e: e.dma_start(T.wsx[:], T.ws[:, :]), [], ["wsx"])
    dma("s", lambda e: e.dma_start(T.vt0[:], T.v[:, :]), [], ["vt0"])

    zero("z0", [], ["z0"])
    z_ke = [clear("ke0", 2048, "z.ke0"), clear("ke1", 2048, "z.ke1")]
    zero("rb", [], ["rb"])
    op("v", lambda e: e.memset(T.half[:], 0.5), [], ["half"])
    for j, w in ((56, -0.5), (57, 0.5), (58, 1.0), (59, 2.0), (60, 3.0)):
        op("v", lambda e: e.memset(V("cf", j, j + 1), w), [], ["cf.%d" % j])
    for n in ("dtl", "ct", "ct2", "cc"):
        z = clear(n, 1024, "z." + n)
        for l in lanes(n):
            wrote[l] = wrote[z[0]]
    dma("a", lambda e: e.dma_start(V("kt", 2560, 3584), V("z0", 0, 1024)), ["z0"], ["z.kt"])
    z_kt = ["z.kt"]
    for n in ("vt", "et"):
        z = clear(n, 512, "z." + n)
        for l in lanes(n) + [n]:
            wrote[l] = wrote[z[0]]
    z_hw = clear("hw", 4096, "z.hw")
    for b in range(4):
        for a in range(4):
            wrote["hw.%d.%d" % (b, a)] = wrote[z_hw[b]]

    iota("ci", 0, 1, [[0, 1]], 0, 1)
    iota("jm", 0, 256, [[0, 16], [1, 16]])
    iota("qlf", 0, 32, [[0, 8], [4, 4]])
    iota("ulf", 0, 8, [[16, 8]])
    iota("ulf", 8, 16, [[32, 4], [-16, 2]], 16)
    iota("ulf", 16, 24, [[-64, 2], [16, 4]], 64)
    iota("gx", 0, 128, [[1, 8], [0, 16]])
    op("g", lambda e: e.iota(V("gx", 13, 128, 16), [[2, 4], [-1, 2]], 1, 0, allow_small_or_imprecise_dtypes=True), [], ["gx"])
    op("g", lambda e: e.iota(V("gx", 14, 128, 16), [[-4, 2], [1, 4]], 4, 0, allow_small_or_imprecise_dtypes=True), [], ["gx"])
    iota("jd", 0, 128, [[1, 8], [0, 16]])
    iota("t16", 0, 16, [[16, 16]])
    iota("jrow", 0, 256, [[1, 256]])
    iota("ev", 0, 256, [[1, 256]])
    iota("gc", 0, 128, [[0, 2], [1, 2], [0, 32]])
    iota("coff", 0, 64, [[1024, 4], [1, 16]])
    iota("vlf", 0, 8, [[0, 2], [1, 2], [8, 2]])
    iota("vr", 0, 64, [[0, 16], [1, 2], [0, 2]], 0)
    iota("vr", 64, 128, [[0, 16], [1, 2], [0, 2]], 2)
    for a in range(4):
        for h in range(2):
            iota("wlf", 32 * a + h, 32 * a + 32, [[128, 4], [0, 2], [32, 2]], 64 * (a >> 1) + 16 * (a & 1), 0, 2)

    def bits(j, sh, m):
        op("v", lambda e: e.tensor_scalar(V("ci", j, j + 1), V("ci", 0, 1), sh, m, A.logical_shift_right, A.bitwise_and), ["ci"], ["ci." + str(j)], True)
    for j, sh, m in ((1, 0, 15), (2, 4, 7), (3, 4, 1), (4, 6, 1), (5, 5, 1), (6, 5, 1), (7, 0, 3), (8, 0, 1), (9, 2, 3)):
        bits(j, sh, m)
    ci_all = ["ci"] + ["ci." + str(j) for j in range(1, 10)]
    vc(V("cf", 0, 10), V("ci", 0, 10), ci_all, ["cf"])

    def cf(j):
        return V("cf", j, j + 1)

    def lin(out, in0, s1, o0, s2, o1, rd, wr, free=False):
        if o0 == A.mult and (o1 is None or o1 == A.add):
            if s2 is None:
                op("a", lambda e: e.activation(out, in0, AF.Copy, scale=s1), rd, wr, free)
            else:
                op("a", lambda e: e.activation(out, in0, AF.Identity, bias=s2, scale=s1), rd, wr, free)
        elif o0 == A.add and o1 is None:
            op("a", lambda e: e.activation(out, in0, AF.Identity, bias=s1, scale=1.0), rd, wr, free)
        else:
            ts(out, in0, s1, o0, s2, o1, rd, wr, free)

    def cs_(j, i, s1, o0, s2=None, o1=None, rd=()):
        lin(cf(j), cf(i), s1, o0, s2, o1, ["cf"] + list(rd), ["cf.%d" % j])


    ts(V("oh", 0, 16), V("jm", 0, 16), cf(1), A.is_equal, None, None, ["jm", "cf"], ["oh"])
    ts(V("mask", 0, 256), V("jm", 0, 256), cf(1), A.is_equal, None, None, ["jm", "cf"], ["mask"])
    ts(V("rst", 0, 256), V("jm", 0, 256), 0.5, A.is_ge, None, None, ["jm"], ["rst"])
    ts(V("pen", 0, 256), V("jm", 0, 256), cf(1), A.is_gt, 1e29, A.mult, ["jm", "cf"], ["pen"])
    vc(V("ul", 0, 24), V("ulf", 0, 24), ["ulf"], ["ul"])
    ts(V("l15", 0, 16), V("t16", 0, 16), 15.0, A.add, None, None, ["t16"], ["l15"])
    ts(V("blkx", 0, 128), V("gx", 0, 128), cf(2), A.is_equal, None, None, ["gx", "cf"], ["blkx"])
    ts(V("kc", 0, 128), V("gx", 0, 128), cf(2), A.is_equal, None, None, ["gx", "cf"], ["kc"])
    ts(V("kc", 11, 128, 16), V("gx", 11, 128, 16), cf(2), A.is_equal, -1.0, A.mult, ["gx", "cf"], ["kc"])
    ts(V("kp", 0, 128), V("jd", 0, 128), cf(2), A.is_equal, None, None, ["jd", "cf"], ["kp"])
    vc(V("lku", 0, 48), V("lki", 0, 48), ["lki"], ["lku"])
    quant("uq", "us", 0, 128, "ut", ["ut"], ["uq"])
    op("v", lambda e: e.tensor_copy(V("up", 0, 384).bitcast(dt.uint32), V("uq", 0, 128).bitcast(dt.uint32).indirect(V("ul", 0, 24))), ["uq", "ul"], ["up"])
    op("a", lambda e: e.activation(V("ups", 0, 384), ind("us", 0, 128, "ul", 0, 24), AF.Copy), ["uq", "ul"], ["ups"])
    quant("xq", "xs", 0, 256, "xt", ["xt"], ["xq"])
    c55 = []

    def setup_unpack(a):
        n = "ke%d" % (a % 2)
        quant("keq", "kes", 512 * a, 512 * a + 512, n, z_ke[a % 2] + lanes(n), ["keq.%d" % a])

    def tiles_unpack(a):
        n = "ke%d" % (a % 2)
        for b in range(4):
            for h in range(2):
                o = 512 * b + b + 256 * h
                op("g", lambda e: e.affine_select(V(n, o, 512 * b + 256 * h + 256, 4), V("half", 0, 64), [[-32, 2], [0, 2], [-1, 16]], A.is_equal, 0.0,
                                                  -(64 * (a >> 1) + 16 * (a & 1)), 1), ["half"] + z_ke[a % 2], ["%s.%d" % (n, b)], True)
    tiles_unpack(0)
    tiles_unpack(1)

    def scores():
        for bank, c in ((0, 0), (6, 0), (4, 1), (5, 2)):
            mm(bank, 256, "up", "ups", 128 * c, "xq", "xs", 0, True, True, ["up", "ups", "xq"])
        for bank, n in ((6, "sw0"), (4, "sw1"), (5, "sw2")):
            act(V(n, 0, 256), V("pb%d" % bank, 0, 256), ["pb%d" % bank], [n])

    def far_scores():
        for k in range(3):
            act(V("n%d" % k, 0, 256), ind("sw%d" % k, 0, 256, "lku", 16 * k, 16 * k + 16), ["sw%d" % k, "lku"], ["n%d" % k])

    def setup_late():
        oh = lambda a, b: V("oh", a, b)
        cs_(49, 7, 16.0, A.mult, cf(9), A.add)
        ts(V("ql", 0, 32), V("qlf", 0, 32), cf(49), A.add, None, None, ["qlf", "cf.49"], ["ql"])
        cs_(28, 3, 256.0, A.mult)
        cs_(29, 3, -256.0, A.mult, 256.0, A.add)
        cs_(30, 28, 512.0, A.add, rd=["cf.28"])
        cs_(6, 4, 512.0, A.mult, cf(28), A.add, ["cf.28"])
        cs_(24, 4, 512.0, A.mult, cf(29), A.add, ["cf.29"])
        cs_(8 + 24, 4, -512.0, A.mult, cf(30), A.add, ["cf.30"])
        cs_(33, 6, -0.5 * OFF, A.add, rd=["cf.6"])
        cs_(34, 5, 512.0, A.mult)
        cs_(26, 1, 64.0, A.mult)
        cs_(27, 6, 1.0 / 256.0, A.mult, rd=["cf.6"])
        cs_(35, 8, 16.0, A.mult)
        cs_(36, 9, 2.0, A.mult, cf(35), A.add, ["cf.35"])
        vc(V("lkf", 0, 48), V("lki", 0, 48), ["lki"], ["lkf"])
        ts(V("m0", 0, 16), V("t16", 0, 16), cf(1), A.add, cf(6), A.add, ["t16", "cf", "cf.6"], ["m0"])
        for k, j in ((0, 6), (1, 24), (2, 32)):
            ts(V("lkx", 16 * k, 16 * k + 16), V("lkf", 16 * k, 16 * k + 16), cf(j), A.add, None, None, ["lkf", "cf.%d" % j], ["lkx"], True)
        ts(V("lkx", 48, 64), V("t16", 0, 16), cf(1), A.add, cf(6), A.add, ["t16", "cf", "cf.6"], ["lkx"], True)
        tt(V("lt0", 0, 256), ind("jrow", 0, 256, "lku", 0, 16), V("ev", 0, 256), A.is_lt, ["jrow", "ev", "lku"], ["lt0"])
        vc(V("ci", 10, 11), V("ci", 5, 6), ["ci.5"], ["ci.10"])
        ts(V("ci", 11, 12), V("ci", 5, 6), 2.0, A.add, None, None, ["ci.5"], ["ci.11"])
        dma("s", lambda e: e.dma_start(T.tbl[:], T.lkx[:]), ["lkx"], ["tbl"])
        for h in range(2):
            dma("g", lambda e: e.indirect_dma_start(V("l4", 2048 * h, 2048 * h + 2048), None, T.tbl[:], IndirectOffsetOnAxis(ap=V("ci", 10 + h, 11 + h), axis=0), bounds_check=3),
                ["tbl", "ci.%d" % (10 + h)], ["l4.%d" % h])
        for j, a in ((19, 0), (20, 4), (21, 8), (31, 12)):
            op("v", lambda e: e.tensor_reduce(cf(j), oh(a, a + 3), AxisListType.X, A.add), ["oh"], ["cf.%d" % j], True)
        c = lambda *js: ["cf.%d" % j for j in js]
        cs_(22, 21, cf(31), A.add, oh(3, 4), A.add, c(21, 31) + ["oh"])
        cs_(37, 22, -0.5, A.add, rd=c(22))
        lin(cf(11), oh(7, 8), -2.0, A.mult, cf(37), A.add, ["oh"] + c(37), c(11))
        lin(cf(12), oh(11, 12), -1e4, A.mult, 1e4, A.add, ["oh"], c(12))
        edge = 127.0 + OFF
        cs_(38, 22, oh(7, 8), A.add, edge + 200.0, A.mult, c(22) + ["oh"])
        cs_(39, 38, -200.0, A.add, rd=c(38))
        lin(cf(13), oh(11, 12), 200.0 - edge, A.mult, cf(39), A.add, ["oh"] + c(39), c(13))
        tt(V("mm3", 0, 3), oh(0, 3), oh(8, 11), A.add, ["oh"], ["mm3.0"])
        tt(V("mm3", 4, 7), oh(4, 7), oh(8, 11), A.add, ["oh"], ["mm3.1"])
        tt(cf(40), oh(3, 4), oh(7, 8), A.add, ["oh"], c(40))
        cs_(48, 20, -1.0, A.mult, rd=c(20))
        cs_(41, 19, 8.0, A.mult, cf(48), A.add, c(19, 48))
        cs_(42, 21, 7.0, A.mult, cf(41), A.add, c(21, 41))
        lin(cf(43), oh(11, 12), 8.0, A.mult, cf(42), A.add, ["oh"] + c(42), c(43))
        R = lambda a, b, st=1: V("rb", a, b, st)

        def put(out, in0, s1, o0, s2=None, o1=None, rd=()):
            lin(out, in0, s1, o0, s2, o1, ["oh", "rb"] + list(rd), ["rb.x"], True)
        m3 = V("mm3", 4, 7)
        put(R(0, 3), V("mm3", 0, 3), -1.0, A.mult, rd=["mm3.0"])
        for base in (0, 64):
            put(R(base + 4, base + 7), m3, -1.0, A.mult, cf(40), A.add, ["mm3.1"] + c(40))
        put(R(8, 11), m3, 3.0, A.mult, cf(43), A.add, ["mm3.1"] + c(43))
        put(R(12, 15), m3, 3.0, A.mult, cf(43), A.add, ["mm3.1"] + c(43))
        cs_(44, 19, cf(21), A.add, oh(11, 12), A.add, c(19, 21) + ["oh"])
        put(R(3, 4), cf(44), 1.0, A.mult, rd=c(44))
        cs_(45, 20, cf(21), A.add, -1.0, A.mult, c(20, 21))
        cs_(46, 40, 3.0, A.mult, cf(45), A.add, c(40, 45))
        put(R(7, 8), oh(11, 12), 8.0, A.mult, cf(46), A.add, c(46))
        put(R(11, 12), oh(11, 12), -1.0, A.mult)
        put(R(64, 67), V("mm3", 0, 3), -1.0, A.mult, oh(11, 12), A.add, ["mm3.0"])
        put(R(72, 75), V("mm3", 0, 3), -1.0, A.mult, rd=["mm3.0"])
        put(R(128, 131), oh(8, 11), -1.0, A.mult)
        put(R(132, 135), oh(4, 7), -1.0, A.mult)
        cs_(47, 21, 8.0, A.mult, cf(48), A.add, c(21, 48))
        put(R(136, 139), oh(4, 7), 3.0, A.mult, cf(47), A.add, c(47))
        put(R(140, 143), oh(4, 7), 3.0, A.mult, cf(47), A.add, c(47))
        put(R(131, 132), cf(21), 1.0, A.mult, rd=c(21))
        put(R(135, 136), cf(20), -1.0, A.mult, rd=c(20))
        far = oh(12, 15)

        def put(out, in0, s1, o0):
            ts(out, in0, s1, o0, None, None, ["oh", "rb"], ["rb.v"], True)
        for j in (8, 9, 10, 12, 13, 14):
            for base in (0, 128):
                put(R(base + 16 + j, base + 64, 16), far, -9.0 if base == 0 else 8.0, A.mult)
        for base, j, w in ((0, 3, -1.0), (0, 7, -1.0), (128, 3, 1.0)):
            put(R(base + 16 + j, base + 64, 16), far, w, A.mult)
        for base, j, w in ((0, 0, 1.0), (0, 4, -1.0), (64, 0, 1.0), (64, 4, -1.0), (64, 8, 1.0), (128, 0, -1.0)):
            put(R(base + 16 + j, base + 64, 17), far, w, A.mult)
        for j in (8, 12):
            ts(R(16 + j, 64, 17), far, -6.0, A.mult, None, None, ["oh", "rb", "rb.v"], ["rb.v"])
        prev = None
        for i, (q, w) in enumerate([(8, 1.0), (9, 2.0), (10, 4.0), (4, 8.0), (5, 16.0), (6, 32.0)]):
            j = 50 + i
            lin(cf(j), oh(q, q + 1), w, A.mult, cf(prev) if prev else None, A.add if prev else None, ["oh"] + (c(prev) if prev else []), c(j))
            prev = j
        c55.append(prev)
        for b in range(4):
            act(V("kt", b, 512, 4), V("kc", 0, 128), ["kc"], ["kt.o%d" % b])
            act(V("kt", 512 + b, 1024, 4), V("kp", 0, 128), ["kp"], ["kt.p%d" % b])
        for b in range(4):
            act(V("bx4", b, 512, 4), V("blkx", 0, 128), ["blkx"], lanes("bx4", b))

    def setup_bits():
        for i, m in enumerate(("s", "fin", "init")):
            o = 4 * K[m]
            tt(V("kt", o, o + 512), ind("rb", 64 * i, 64 * i + 64, "ql", 0, 32), V("bx4", 0, 512), A.mult, ["rb.x", "rb.v", "ql"] + lanes("bx4"), ["kt." + m])
        quant("kq", "ks", 256, 640, "kt", ["kt.s", "kt.fin", "kt.init"], ["kq"], 1024)

    def setup_routes():
        c = lambda *js: ["cf.%d" % j for j in js]
        o = 4 * K["kw"]
        ts(V("vm", 0, 128), V("gc", 0, 128), cf(5), A.is_equal, 16.0, A.mult, ["gc", "cf"], ["vm.t"])
        tt(V("kt", o, o + 512, 4), V("vm", 0, 128), V("mask", 0, 128), A.mult, ["vm.t", "mask"] + z_kt, ["kt.w0"])
        lin(V("kt", o + 2, o + 512, 4), V("kt", o, o + 512, 4), 2.0, A.mult, None, None, ["kt.w0"] + z_kt, ["kt.w2"])
        ts(V("vm", 0, 128), V("vr", 0, 128), cf(27), A.is_equal, None, None, ["vr", "cf.27"], ["vm", "vm.t"])
        prev = c55[0]
        o = 4 * K["nd"]
        ts(V("kt", o, o + 512, 4), V("jd", 0, 128), cf(2), A.is_equal, cf(prev), A.mult, ["jd", "cf"] + z_kt + c(prev), ["kt.n0"])
        quant("kq", "ks", 640, 896, "kt", z_kt + ["kt.w0", "kt.w2", "kt.n0"], ["kq.2"], 2560)
        lin(V("coff", 0, 64), V("coff", 0, 64), 1.0, A.mult, cf(26), A.add, ["coff", "cf.26"], ["coff"])
        ts(V("vl", 0, 8), V("vlf", 0, 8), cf(36), A.add, None, None, ["vlf", "cf.36"], ["vl"])

    def setup_zero():
        quant("zq", "zs", 0, 128, "z0", ["z0"], ["zq"])
        quant("vq", "vs", 0, 128, "vt0", ["vt0"], ["vq"])
        for t in range(ROUNDS):
            dma("s", lambda e: e.dma_start(V("aq%d" % t, GW, 128).bitcast(dt.uint8), V("zq", GW, 128).bitcast(dt.uint8)), ["zq"], ["aq%d" % t])
            dma("s", lambda e: e.dma_start(V("as%d" % t, GW, 128), V("zs", GW, 128)), ["zq"], ["as%d" % t])

    def layers():
        op("v", lambda e: e.tensor_copy(V("wp", 0, 2048).bitcast(dt.uint32), V("wq", 0, 512).bitcast(dt.uint32).indirect(V("wl", 0, 128))), ["wq", "wl"], ["wp"])
        op("a", lambda e: e.activation(V("wps", 0, 2048), ind("wsx", 0, 512, "wl", 0, 128), AF.Copy), ["wsx", "wl"], ["wps"])

    hw_lanes = ["hw.%d.%d" % (b, a) for b in range(4) for a in range(4)]

    def pick(n, off, oa, ob, dst, dst_at, name):
        rd = ["da.0", "da.1"] if n == "da" else [n + ".0", n + ".1"]
        tt(V("hp", 0, 256), ind(n, 0, 1024, off, oa, ob), V("mask", 0, 256), A.mult, rd + ["mask", name], ["hp"])
        op("v", lambda e: e.tensor_tensor_scan(V("hs", 0, 256), V("rst", 0, 256), V("hp", 0, 256), 0.0, A.mult, A.add), ["rst", "hp"], ["hs"])
        vc(V(dst, dst_at, dst_at + 16), V("hs", 15, 256, 16), ["hs"], [dst + ".%d" % dst_at])

    fw_lanes = ["fw.%d.%d" % (b, a) for b in range(4) for a in range(4)]

    unpacked = [0]

    def unpack_products(k):
        for i in range(unpacked[0], unpacked[0] + k):
            a, b, bank = i // 4, i % 4, 4 + (i + 3) % 4
            mm(bank, 256, "keq", "kes", 512 * a + 128 * b, "xq", "xs", 0, True, True, ["keq.%d" % a, "xq"])

    def unpack_casts(k):
        for i in range(unpacked[0], unpacked[0] + k):
            a, b, bank = i // 4, i % 4, 4 + (i + 3) % 4
            o = 1024 * b + 256 * a
            act(V("fw", o, o + 256), V("pb%d" % bank, 0, 256), ["pb%d" % bank], ["fw.%d.%d" % (b, a)])
        unpacked[0] = (unpacked[0] + k) % 16

    def d_start():
        ts(V("dh", 0, 256), V("pb2", 0, 256), cf(11), A.is_ge, cf(12), A.mult, ["pb2", "cf.11", "cf.12"], ["dh"])
        act(V("dh2", 0, 256), V("dh", 0, 256), ["dh", "cf.13"], ["dh2"], bias=cf(13))

    dst = T.cores[(rank + 1) % N]
    via = helper_of(topo, core, dst)

    for t in range(ROUNDS):
        last = t == ROUNDS - 1
        if t == 0:
            setup_late()
        scores()
        tt(V("so", 0, 256), V("pb0", 0, 256), V("mask", 0, 256), A.mult, ["pb0", "mask"], ["so"])
        op("v", lambda e: e.tensor_tensor_scan(V("wsc", 0, 256), V("rst", 0, 256), V("so", 0, 256), 0.0, A.mult, A.add), ["rst", "so"], ["wsc"])
        tt(V("wm", 0, 256), ind("wsc", 0, 256, "l15", 0, 16), V("pen", 0, 256), A.add, ["wsc", "l15", "pen"], ["wm"])
        tt(V("so", 0, 256), V("pb0", 0, 256), V("wm", 0, 256), A.not_equal, ["pb0", "wm"], ["so"])
        act(V("dtl", 0, 1024, 4), V("so", 0, 256), ["so"], ["dtl.0"], scale=2.0)
        for c in ON_SCALAR:
            el, n, s = c % 4, "cm%d" % {2: 3, 3: 2}[c // 4], 256 * (c % 4)
            sc, sg = V("wsc", 16 * c + 15, 16 * c + 16), V("sg", s, s + 256)
            op("a", lambda e: e.activation(sg, V("sw0", 0, 256), AF.Sign, bias=sc, scale=-1.0), ["sw0", "wsc"], ["sg.%d" % el])
            op("a", lambda e: e.activation(V(n, el, 64 * c, 4), V("sg", s, s + 16 * c), AF.Sign, bias=cf(56), scale=-1.0), ["sg.%d" % el, "cf.56"], ["%s.%dl" % (n, el)])
            op("a", lambda e: e.activation(V(n, 64 * c + el, 1024, 4), V("sg", s + 16 * c, s + 256), AF.Sign, bias=cf(57), scale=-1.0), ["sg.%d" % el, "cf.57"], ["%s.%dr" % (n, el)])
        far_scores()
        if t:
            unpack_products(4)
            unpack_casts(4)
        kinds = (("own", 1), ("pl", 3))
        for step, tile in enumerate((0, 4, 1, 2, 3)):
            n = "cm%d" % (tile if tile < 2 else {2: 3, 3: 2, 4: 9}[tile])
            for el in range(4 if tile < 4 else 0):
                c = 4 * tile + el
                if c in ON_SCALAR:
                    continue
                sc = V("wsc", 16 * c + 15, 16 * c + 16)
                if c:
                    ts(V(n, el, 64 * c, 4), V("pb0", 0, 16 * c), sc, A.is_gt, 2.0, A.mult, ["pb0", "wsc"], ["%s.%dl" % (n, el)])
                ts(V(n, 64 * c + el, 1024, 4), V("pb0", 16 * c, 256), sc, A.is_ge, 2.0, A.mult, ["pb0", "wsc"], ["%s.%dr" % (n, el)])
            if t == 0 and step == 0:
                quant("kq", "ks", 0, 256, "kt", ["kt.%s%d" % (x, b) for x in "op" for b in range(4)], ["kq.1"])
            if tile == 4:
                quant("cq", "cs", 1024, 1280, "dtl", lanes("dtl"), ["cq.4"])
            else:
                quant("cq", "cs", 256 * tile, 256 * tile + 256, n, ["%s.%d%s" % (n, el, s) for el in range(4) for s in "lr"], ["cq.%d" % tile])
            for m, bank in kinds:
                mm(bank, 256, "kq", "ks", K[m], "cq", "cs", 256 * tile, step == 0, step == 4, ["kq.1", "cq.%d" % tile])
            if t == 0 and tile == 1:
                setup_unpack(0)
                setup_unpack(1)
                tiles_unpack(2)
                tiles_unpack(3)
            if t == 0 and tile == 2:
                setup_bits()
                for k in range(3):
                    nk = V("n%d" % k, 0, 256)
                    tt(V("ct", 1 + k, 1024, 4), nk, V("pb0", 0, 256), A.is_lt, ["pb0", "n%d" % k], lanes("ct", 1 + k))
                    tt(V("ct2", 1 + k, 1024, 4), nk, V("pb0", 0, 256), A.is_equal, ["pb0", "n%d" % k], lanes("ct2", 1 + k))
                l = V("ct2", 1, 1024, 4)
                for k, j in ((1, 3), (2, 4)):
                    l2 = V("ct2", 1 + k, 1024, 4)
                    act(l2, l2, lanes("ct2", 1 + k) + ["cf"], lanes("ct2", 1 + k), scale=cf(j))
                tt(l, l, V("lt0", 0, 256), A.mult, lanes("ct2", 1) + ["lt0"], lanes("ct2", 1))
                for i, n2 in enumerate(("ct", "ct2")):
                    quant("ctq", "cts", 256 * i, 256 * i + 256, n2, lanes(n2), ["ctq.%d" % i])
                    mm(2, 256, "kq", "ks", K["init"], "ctq", "cts", 256 * i, i == 0, i == 1, ["kq", "ctq.%d" % i])
                d_start()
        tt(V("bw", 0, 256), V("pb1", 0, 256), V("dh2", 0, 256), A.is_gt, ["pb1", "dh2"], ["bw"])

        def fill_mask():
            tt(V("r1", 0, 256), V("pb3", 0, 256), V("mask", 0, 256), A.mult, ["pb3", "mask"], ["r1"])
            act(V("rr", 0, 256), V("pb3", 0, 256), ["pb3", "cf.33"], ["rr"], scale=0.5, bias=cf(33))

        def fill_wrap():
            op("v", lambda e: e.tensor_tensor_scan(V("r2", 0, 256), V("rst", 0, 256), V("r1", 0, 256), 0.0, A.mult, A.add), ["rst", "r1"], ["r2"])
            ts(V("mu", 96, 112), V("r2", 15, 256, 16), 0.5, A.mult, -0.5 * OFF, A.add, ["r2"], ["mu.96"])

        def fill_places():
            dma("s", lambda e: e.dma_start(T.tbh[:], T.rr[0:128:16, :]), ["rr"], ["tbh"])
            for h in range(2):
                dma("g", lambda e: e.indirect_dma_start(V("ho", 512 * h, 512 * h + 512), None, T.tbh[:], IndirectOffsetOnAxis(ap=V("ci", 10 + h, 11 + h), axis=0), bounds_check=3),
                    ["tbh", "ci.%d" % (10 + h)], ["ho.%d" % h])
            op("v", lambda e: e.tensor_copy(V("lw", 0, 256).indirect(V("mu", 96, 112)), V("jrow", 0, 256)), ["mu.96", "jrow"], ["lw"])

        def fill_list():
            tt(V("r1", 0, 64), V("lw", 0, 64), V("mask", 0, 64), A.mult, ["lw", "mask"], ["r1"])
            op("v", lambda e: e.tensor_tensor_scan(V("r2", 0, 64), V("rst", 0, 64), V("r1", 0, 64), 0.0, A.mult, A.add), ["rst", "r1"], ["r2"])
            ts(V("mu", 112, 116), V("r2", 15, 64, 16), cf(6), A.add, None, None, ["r2", "cf.6"], ["mu.112"])

        def fill_gate():
            for b in range(4):
                act(V("et", b, 256, 4), ind("fw", 1024 * b, 1024 * b + 1024, "mu", 112, 116), fw_lanes + ["mu.112"], lanes("et", b), scale=2.0)

        def fill_send():
            quant("eq%d" % t, "es%d" % t, 0, 128, "et", lanes("et"), ["eq%d" % t])
            waits("g", ["eq%d" % t], [])
            to = dst if via is None else via
            p = "a" if via is None else "r"
            send(g, T, topo, core, to, V("%sq%d" % (p, t), 0, GW), V("eq%d" % t, 0, GW), V("%ss%d" % (p, t), 0, GW), V("es%d" % t, 0, GW),
                 T.sem["%s%d" % ("arr" if via is None else "rel", t)])

        def fill_turn(k):
            op("v", lambda e: e.transpose(V("nt%d" % k, 0, 256), V("n%d" % k, 0, 256)), ["n%d" % k], ["nt%d" % k])

        def fill_pref():
            nt = [V("nt%d" % k, 0, 256, 16) for k in range(3)]
            P = lambda i: V("pw", 16 * i, 16 * i + 16)
            for i, (x, y) in enumerate(((0, 1), (0, 2), (1, 2))):
                tt(P(3 + i), nt[x], nt[y], A.is_le, ["nt%d" % x, "nt%d" % y], ["pw.%d" % (3 + i)])

        def fill_weigh():
            P = lambda i: V("pw", 16 * i, 16 * i + 16)
            tt(P(0), P(3), P(4), A.add, ["pw.3", "pw.4"], ["pw.0"])
            tt(P(1), P(5), P(3), A.subtract, ["pw.5", "pw.3"], ["pw.1"])
            tt(P(2), P(4), P(5), A.add, ["pw.4", "pw.5"], ["pw.2"])
            for k, w, j in ((0, 1.0, 58), (1, 1.0, 59), (2, -1.0, 60)):
                act(P(k), P(k), ["pw.%d" % k, "cf.%d" % j], ["pw.%d" % k], scale=w, bias=cf(j))
        before = [[fill_mask], [lambda: fill_turn(0)], [lambda: fill_turn(1)], [lambda: fill_turn(2)], [], [fill_send]]
        after = [[fill_wrap], [fill_places], [fill_list], [fill_pref], [fill_gate, fill_weigh], []]
        some = (4, 4, 4, 4) if t == 0 else (3, 3, 3, 3)

        for i in range(SWEEPS):
            if i < 4:
                unpack_products(some[i])
            vc(V("st", 0, 1024, 4), V("bw", 0, 256), ["bw"], lanes("st", 0))
            for k in (1, 2):
                act(V("st", 1 + k, 1024, 4), ind("bw", 0, 256, "lku", 16 * k, 16 * k + 16), ["bw", "lku"], lanes("st", 1 + k))
            vc(V("st", 1, 1024, 4), ind("bw", 0, 256, "lku", 0, 16), ["bw", "lku"], lanes("st", 1))
            if i < 4:
                unpack_casts(some[i])
            for f in before[i]:
                f()
            quant("sq", "ss", 0, 256, "st", lanes("st"), ["sq"])
            m = "fin" if i == SWEEPS - 1 else "s"
            mm(2, 256, "kq", "ks", K[m], "sq", "ss", 0, True, True, ["kq", "kq.2", "sq"])
            if t == 0 and i < 2:
                setup_unpack(2 + i)
            for f in after[i]:
                f()
            if t == 0:
                if i == 1:
                    setup_zero()
                if i == 4:
                    ts(V("wl", 0, 128), V("wlf", 0, 128), cf(1), A.add, None, None, ["wlf", "cf"], ["wl"])
                    layers()
                if i == 5:
                    setup_routes()
            ts(V("bw", 0, 256), V("pb2", 0, 256), cf(11) if m == "s" else -0.5, A.is_lt, None, None, ["pb2", "cf.11"], ["bw"])
        op("v", lambda e: e.transpose(V("bt", 0, 256), V("bw", 0, 256)), ["bw"], ["bt"])
        tk = lambda i: V("tk", 16 * i, 16 * i + 16)
        for k in range(3):
            tt(tk(k), V("bt", k, 256, 16), V("pw", 16 * k, 16 * k + 16), A.mult, ["bt", "pw.%d" % k], ["tk.%d" % k])
        tt(tk(3), tk(0), tk(1), A.max, ["tk.0", "tk.1"], ["tk.3"])
        tt(tk(4), tk(3), tk(2), A.max, ["tk.3", "tk.2"], ["tk.4"])
        for i in range(2):
            tt(V("eqk", 16 * i, 16 * i + 16), tk(1 + i), tk(4), A.is_equal, ["tk.%d" % (1 + i), "tk.4"], ["eqk.%d" % i])
        tt(V("vt", 0, 256, 2), ind("eqk", 0, 32, "vl", 0, 8), V("vm", 0, 128), A.mult, ["eqk.0", "eqk.1", "vl", "vm"], ["vt"])
        quant("vtq", "vts", 0, 128, "vt", ["vt"], ["vtq"])
        mm(0, 128, "kq", "ks", K["kw"], "vtq", "vts", 0, True, True, ["kq.2", "vtq"])
        act(V("cc", 0, 1024, 4), V("bw", 0, 256), ["bw"], lanes("cc", 0))
        quant("ccq", "ccs", 0, 256, "cc", lanes("cc"), ["ccq"])
        if not last:
            mm(2, 256, "kq", "ks", K["init"], "ccq", "ccs", 0, True, True, ["kq", "ccq"])
        tt(V("of", 0, 64), V("pb0", 0, 64), V("coff", 0, 64), A.add, ["pb0", "coff"], ["of"])
        vc(V("ou", 0, 64), V("of", 0, 64), ["of"], ["ou"])
        l4 = ["l4.0", "l4.1"]
        op("a", lambda e: e.activation(V("da", 512, 1024), ind("l4", 0, 4096, "ou", 32, 64), AF.Copy), l4 + ["ou"], ["da.1"])
        vc(V("da", 0, 512), ind("l4", 0, 4096, "ou", 0, 32), l4 + ["ou"], ["da.0"])
        if True:
            Q["t"].wait_ge(T.sem["arr%d" % t], 2 * NE)
        pick("da", "m0", 0, 16, "mu", 0, "m0")
        for b in range(4):
            act(V("fd", 256 * b, 256 * b + 256), ind("fw", 1024 * b, 1024 * b + 1024, "mu", 0, 16), fw_lanes + ["mu.0"], ["fd.%d" % b])
        i = 0
        for a in range(4):
            for b in range(4):
                bank = 4 + i % 4
                mm(bank, 128, "wp", "wps", 512 * a + 128 * b, "aq%d" % t, "as%d" % t, 0, True, True, ["wp", "wps", "aq%d" % t, "as%d" % t])
                o = 1024 * b + 256 * a
                act(V("hw", o, o + GW), V("pb%d" % bank, 0, GW), ["pb%d" % bank], ["hw.%d.%d" % (b, a)], scale=0.015625)
                i += 1
        if not last:
            d_start()
        pick("da", "mu", 0, 16, "mu", 16, "mu.0")
        pick("da", "mu", 16, 32, "mu", 32, "mu.16")
        pick("da", "mu", 32, 48, "mu", 48, "mu.32")
        pick("ho", "mu", 48, 64, "mu", 64, "mu.48")
        for b in range(4):
            tt(V("zb", 256 * b, 256 * b + 256), ind("fw", 1024 * b, 1024 * b + 1024, "mu", 48, 64), V("fd", 256 * b, 256 * b + 256), A.add,
               fw_lanes + ["mu.48", "fd.%d" % b], ["zb.%d" % b])
        for b in range(4):
            tt(V("xn", b, 1024, 4), ind("hw", 1024 * b, 1024 * b + 1024, "mu", 64, 80), V("zb", 256 * b, 256 * b + 256), A.add,
               hw_lanes + ["mu.64", "zb.%d" % b], lanes("xn", b))
        quant("xq", "xs", 0, 256, "xn", lanes("xn"), ["xq"])
        if last:
            dma("s", lambda e: e.dma_start(T.oc[:, :], T.xq[:].bitcast(dt.uint8)), ["xq"], ["out.oc"])
            for k in range(4):
                dma("s", lambda e: e.dma_start(T.osc[4 * k:4 * k + 4, :], T.xs[32 * k:32 * k + 4, :]), ["xq"], ["out.os%d" % k])
            mm(4, 256, "vq", "vs", 0, "xq", "xs", 0, True, True, ["vq", "xq"])
            mm(5, 256, "kq", "ks", K["nd"], "ccq", "ccs", 0, True, True, ["kq.2", "ccq"])
            act(V("ev", 0, 256), ind("da", 0, 1024, "mu", 32, 48), ["da.0", "da.1", "mu.32"], ["ev.0"])
            act(V("ys", 0, 256), V("pb4", 0, 256), ["pb4"], ["ys"])
            dma("s", lambda e: e.dma_start(T.y[:, :], T.ys[:]), ["ys"], ["out.y"])
            act(V("ndb", 256, 512), V("pb5", 0, 256), ["pb5"], ["ndb.1"])
            ts(V("ev", 256, 512), V("ev", 0, 256), 512.0, A.is_ge, 512.0, A.mult, ["ev.0"], ["ev.1"])
            ts(V("hp", 0, 256), V("ev", 0, 256), cf(34), A.add, None, None, ["ev.0", "cf.34"], ["hp"])
            tt(V("ndb", 0, 256), V("hp", 0, 256), V("ev", 256, 512), A.add, ["hp", "ev.1"], ["ndb.0"])
            dma("s", lambda e: e.dma_start(T.nd[:, :], T.ndb[0:128:16, :]), ["ndb.0", "ndb.1"], ["out.nd"])
    for s in sorted(cnt):
        if known["g"].get(s, 0) < cnt[s]:
            g.wait_ge(T.sem[s], cnt[s])
    g.wait_ge(T.sem.loc, 2 * NE * ROUNDS)
